import numpy as np
import ml_dtypes


def mxq(x, axis, fmt="e4m3"):
    dtype, down = {"e4m3": (ml_dtypes.float8_e4m3fn, 7), "e5m2": (ml_dtypes.float8_e5m2, 14)}[fmt]
    v = np.moveaxis(np.asarray(x, np.float32).astype(ml_dtypes.bfloat16).astype(np.float64), axis, -1)
    blocks = v.reshape(v.shape[:-1] + (-1, 32))
    amax = np.abs(blocks).max(-1, keepdims=True)
    byte = np.maximum(np.where(amax > 0, np.frexp(amax)[1] - 1 + 127, 0) - down, 1)
    scale = np.exp2(byte - 127.0)
    codes = (blocks / scale).astype(np.float32).astype(dtype).astype(np.float64)
    return np.moveaxis((codes * scale).reshape(v.shape), -1, axis)


WIDE = False


def mx_kscale(k):
    if not WIDE:
        return np.ones(k)
    levels = np.array([10, -10, 5, -5, 0])
    if k % 512:
        return np.exp2(np.random.permutation(np.resize(levels, k // 32))).repeat(32)
    a = np.empty((k // 512, 16))
    for p in range(k // 512):
        a[p, :8] = np.random.permutation(np.resize(levels, 8))
        for g in range(8):
            far = levels[np.abs(levels - a[p, g]) >= 10]
            a[p, g + 8] = far[np.random.randint(len(far))]
    return np.exp2(a.ravel()).repeat(32)


def f64(x):
    return np.asarray(x).astype(np.float64)


def striped(idx):
    return np.tile(idx.reshape(-1, 16).T, (8, 1)).astype(np.uint16)


def unstriped(offs):
    return offs[:16].T.reshape(-1).astype(np.int64)


E2M1 = np.array([0.0, 0.5, 1.0, 1.5, 2.0, 3.0, 4.0, 6.0, -0.0, -0.5, -1.0, -1.5, -2.0, -3.0, -4.0, -6.0])


def pack_weight(w, fmt):
    k, n = w.shape
    w = f64(np.asarray(w, np.float32).astype(ml_dtypes.bfloat16)).reshape(k // 32, 32, n)
    amax = np.abs(w).max(1)
    if fmt == "e4m3":
        byte = np.frexp(amax)[1] - 1 + 127 - 7
    else:
        mant, ex = np.frexp(amax / 6.0)
        byte = np.where(mant > 0.5, ex, ex - 1) + 127
    byte = np.clip(np.where(amax > 0, byte, 1), 1, 254)
    scaled = (w * np.exp2(127.0 - byte)[:, None, :]).reshape(k, n).astype(np.float32)
    by_word = np.ascontiguousarray(scaled.reshape(k // 512, 128, 4, n).transpose(0, 1, 3, 2))
    if fmt == "e4m3":
        words = by_word.astype(ml_dtypes.float8_e4m3fn).view(np.uint8)
    else:
        c = by_word.astype(ml_dtypes.float4_e2m1fn).view(np.uint8) & 0xF
        words = (c[..., 0::2] | (c[..., 1::2] << 4)).reshape(k // 512, 128, 2 * n)
    return np.ascontiguousarray(words), np.ascontiguousarray(byte.astype(np.uint8).reshape(k // 512, 16, n))


def unpack_weight(words, scales, fmt):
    g, _, n = scales.shape
    words = np.ascontiguousarray(words).reshape(g, 128, n, -1)
    if fmt == "e4m3":
        vals = words.view(ml_dtypes.float8_e4m3fn).astype(np.float64)
    else:
        nib = np.empty((g, 128, n, 4), np.uint8)
        nib[..., 0::2] = words & 0xF
        nib[..., 1::2] = words >> 4
        vals = E2M1[nib]
    vals = vals * np.repeat(np.exp2(scales.astype(np.float64) - 127.0), 8, axis=1)[..., None]
    return vals.transpose(0, 1, 3, 2).reshape(g * 512, n)


def gelu(v):
    return 0.5 * v * (1.0 + np.tanh(np.sqrt(2.0 / np.pi) * (v + 0.044715 * v**3)))


def striped8(idx):
    return np.concatenate([v.reshape(-1, 16).T for v in idx]).astype(np.uint16)


def unstriped8(offs):
    return np.stack([offs[16 * g:16 * g + 16].T.reshape(-1) for g in range(8)]).astype(np.int64)


def heads(xT, wgt, idx8):
    k = np.arange(xT.shape[0])
    return wgt[k // 4 % 128] * xT[k[:, None], idx8[k % 512 // 64]]


K, T, S, H, N = 1024, 2048, 1024, 1024, 256

def setup_inputs():
    n = np.random.standard_normal
    s = mx_kscale(K)[:, None]
    u = mx_kscale(H)[:, None]
    d = {}
    d["xT"] = (n((K, T)) * s).astype(np.float32)
    d["wgt"] = np.repeat(np.random.uniform(0.5, 2.0, (8, S)), 16, axis=0).astype(np.float32)
    d["offs"] = striped8(np.stack([np.random.permutation(T)[:S] for _ in range(8)]))
    d["w1"] = (n((K, H)) / np.sqrt(K) / s * u.T).astype(np.float32)
    d["b1"] = (0.5 * n(H) * u[:, 0]).astype(np.float32)
    d["w2_words"], d["w2_scales"] = pack_weight(n((K, H)) / np.sqrt(K) / s * u.T, "e2m1")
    d["b2"] = (0.5 * n(H) * u[:, 0]).astype(np.float32)
    d["w3_words"], d["w3_scales"] = pack_weight(n((H, N)) / np.sqrt(H) / u, "e4m3")
    d["b3"] = (0.5 * n(N)).astype(np.float32)
    return d

def reference(xT, wgt, offs, w1, b1, w2_words, w2_scales, b2, w3_words, w3_scales, b3):
    xg = mxq(heads(f64(xT), f64(wgt), unstriped8(offs)), 0, "e4m3")
    w1q = mxq(f64(w1), 0, "e4m3")
    w2 = unpack_weight(w2_words, w2_scales, "e2m1")
    w3 = unpack_weight(w3_words, w3_scales, "e4m3")
    c1 = (w1q.T @ xg) + f64(b1)[:, None]
    c2 = (w2.T @ xg) + f64(b2)[:, None]
    h = mxq(np.maximum(c1, c2), 0, "e4m3")
    return (w3.T @ h) + f64(b3)[:, None]

@@ -1,0 +1,230 @@
+from contextlib import ExitStack
+
+import concourse.mybir as mybir
+
+K, T, S, H, N = 1024, 2048, 1024, 1024, 256
+FLOPS = 2 * S * (2 * K * H + H * N)
+
+F32 = mybir.dt.float32
+BF16 = mybir.dt.bfloat16
+I32 = mybir.dt.int32
+U32 = mybir.dt.uint32
+U16 = mybir.dt.uint16
+U8 = mybir.dt.uint8
+FP8X4 = mybir.dt.float8_e4m3fn_x4
+FP4X4 = mybir.dt.float4_e2m1fn_x4
+MULT = mybir.AluOpType.mult
+ADD = mybir.AluOpType.add
+MAX = mybir.AluOpType.max
+IDENT = mybir.ActivationFunctionType.Identity
+
+P = 128
+PACK = 4
+PASS = P * PACK
+W = 512
+
+
+def tile_list_replay_maxout_values_kernel(
+    tc, xT, wgt, offs, w1, b1, w2_words, w2_scales, b2, w3_words, w3_scales, b3, out
+):
+    nc = tc.nc
+    with ExitStack() as ctx:
+        keep = ctx.enter_context(tc.tile_pool(name="keep", bufs=1))
+        windows = ctx.enter_context(tc.tile_pool(name="windows", bufs=6))
+        ring3 = ctx.enter_context(tc.tile_pool(name="ring3", bufs=3))
+        ring2 = ctx.enter_context(tc.tile_pool(name="ring2", bufs=2))
+        ring4 = ctx.enter_context(tc.tile_pool(name="ring4", bufs=4))
+        psum = ctx.enter_context(tc.psum_pool(name="psum", bufs=8))
+
+        offsets = keep.tile([P, S // 16], U16, name="offsets")
+        wgt_sb = [keep.tile([P, W], F32, name="wgt%d" % s) for s in range(2)]
+        w2_raw = keep.tile([P, 2, 2 * H], U8, name="w2_raw", align_bytes=64)
+        w2_codes = keep.tile([P, 2 * 2 * H], U8, name="w2_codes", align_bytes=64)
+        w2_sraw = keep.tile([P, 2, H], U8, name="w2_sraw", align_bytes=64)
+        w2_plane = keep.tile([P, 2 * H], U8, name="w2_plane", align_bytes=64)
+        w3_codes = keep.tile([P, 2, N], U32, name="w3_codes", align_bytes=64)
+        w3_plane = keep.tile([P, 2, N], U8, name="w3_plane", align_bytes=64)
+        b1_sb = keep.tile([P, 2, PACK], F32, name="b1_sb")
+        b2_sb = keep.tile([P, 2, PACK], F32, name="b2_sb")
+        b3_sb = keep.tile([P, 2], F32, name="b3_sb")
+
+        NCH = {(0, 0): 1, (0, 1): 1, (1, 0): 1, (1, 1): 2}
+        ORDER = [('ld', 'offs'), ('ld', 'w2s'), ('ld', 'w2'), ('ld', 'wgt', 0), ('ld', 'win', 0, 0), ('g', 0, 0, 0), ('ld', 'wgt', 1), ('ld', 'win', 0, 1), ('ld', 'win', 0, 2), ('ld', 'win', 0, 3), ('ld', 'win', 1, 0), ('g', 0, 1, 0), ('ld', 'win', 1, 1), ('g', 1, 0, 1), ('perm', 'w2'), ('g', 0, 0, 1), ('ld', 'win', 1, 2),  ('g', 0, 2, 0), ('g', 0, 1, 1), ('ld', 'win', 1, 3), ('ld', 'w1raw', 0, 0), ('iw', 0, 0, 0), ('g', 1, 1, 1), ('g', 0, 2, 1), ('ld', 'w1raw', 1, 0), ('ld', 'w3'), ('g', 0, 3, 0), ('g', 1, 2, 1), ('g', 1, 3, 1), ('ix', 0, 0, 0), ('iw', 1, 0, 0), ('g', 1, 0, 0), ('perm', 'w2s'), ('ix', 0, 0, 1), ('qx', 0, 0), ('g', 0, 3, 1), ('iw', 0, 0, 1), ('ld', 'w1raw', 0, 1), ('g', 1, 1, 0), ('qw', 0, 0), ('ix', 1, 1, 0), ('ix', 1, 1, 1), ('iw', 1, 0, 1), ('ix', 0, 1, 0), ('ld', 'w1raw', 1, 1), ('g', 1, 2, 0), ('ix', 0, 1, 1), ('qx', 1, 1), ('qx', 0, 1), ('g', 1, 3, 0), ('iw', 1, 1, 0), ('iw', 0, 1, 0), ('qw', 1, 0), ('ix', 1, 0, 0), ('c2', 0, 1), ('ix', 1, 0, 1), ('iw', 1, 1, 1), ('qx', 1, 0), ('qw', 1, 1), ('c2', 0, 0), ('mx', 0, 1, 0), ('mx', 0, 0, 0), ('ih', 0, 1, 0, 0), ('iw', 0, 1, 1), ('ih', 0, 1, 0, 1), ('c2', 1, 0), ('ih', 0, 0, 0, 0), ('qw', 0, 1), ('ih', 0, 0, 0, 1), ('mx', 1, 0, 0), ('ih', 1, 0, 0, 0), ('c2', 1, 1), ('mx', 1, 1, 0), ('ih', 1, 0, 0, 1), ('ih', 1, 1, 0, 0), ('qh', 1, 0, 0), ('mx', 1, 1, 1), ('ih', 1, 1, 1, 0), ('qh', 0, 1, 0), ('ih', 1, 1, 0, 1), ('qh', 1, 1, 0), ('qh', 0, 0, 0), ('ih', 1, 1, 1, 1), ('qh', 1, 1, 1), ('val', 0, 0), ('val', 1, 0), ('val', 1, 1)]
+        ASG = {('ix', 0, 0, 0): 'S', ('iw', 0, 0, 0): 'S', ('ih', 0, 0, 0, 0): 'V', ('ix', 0, 0, 1): 'S', ('iw', 0, 0, 1): 'S', ('ih', 0, 0, 0, 1): 'S', ('c2', 0, 0, 0): 'S', ('c2', 0, 0, 1): 'S', ('c2', 0, 0, 2): 'V', ('c2', 0, 0, 3): 'S', ('val', 0, 0, 0): 'S', ('ix', 0, 1, 0): 'S', ('iw', 0, 1, 0): 'S', ('ih', 0, 1, 0, 0): 'S', ('ix', 0, 1, 1): 'S', ('iw', 0, 1, 1): 'S', ('ih', 0, 1, 0, 1): 'S', ('c2', 0, 1, 0): 'S', ('c2', 0, 1, 1): 'S', ('c2', 0, 1, 2): 'S', ('c2', 0, 1, 3): 'S', ('val', 0, 0, 1): 'V', ('ix', 1, 0, 0): 'V', ('iw', 1, 0, 0): 'V', ('ih', 1, 0, 0, 0): 'V', ('ix', 1, 0, 1): 'V', ('iw', 1, 0, 1): 'S', ('ih', 1, 0, 0, 1): 'S', ('c2', 1, 0, 0): 'S', ('c2', 1, 0, 1): 'S', ('c2', 1, 0, 2): 'S', ('c2', 1, 0, 3): 'S', ('val', 1, 0, 0): 'S', ('val', 1, 1, 0): 'V', ('ix', 1, 1, 0): 'V', ('iw', 1, 1, 0): 'S', ('ih', 1, 1, 0, 0): 'S', ('ih', 1, 1, 1, 0): 'V', ('ix', 1, 1, 1): 'S', ('iw', 1, 1, 1): 'V', ('ih', 1, 1, 0, 1): 'S', ('ih', 1, 1, 1, 1): 'S', ('c2', 1, 1, 0): 'S', ('c2', 1, 1, 1): 'S', ('c2', 1, 1, 2): 'V', ('c2', 1, 1, 3): 'S', ('val', 1, 0, 1): 'V', ('val', 1, 1, 1): 'S'}
+        xT_planes = xT.rearrange("(a p i) t -> a i p t", p=P, i=PACK)
+        w1_rows = w1.rearrange("(a p j) c -> a p j c", p=P, j=PACK)
+        tiles = {}
+
+        def copy_on(engine, dst, src):
+            if engine == "S":
+                nc.scalar.copy(out=dst, in_=src)
+            elif engine == "G":
+                nc.gpsimd.tensor_scalar(out=dst, in0=src, scalar1=1.0, scalar2=0.0, op0=MULT, op1=ADD)
+            else:
+                nc.vector.tensor_copy(out=dst, in_=src)
+
+        def add_bias(engine, dst, acc, bias):
+            if engine == "S":
+                nc.scalar.activation(out=dst, in_=acc, func=IDENT, bias=bias)
+            else:
+                nc.vector.tensor_scalar(out=dst, in0=acc, scalar1=bias, scalar2=None, op0=ADD)
+
+        def load_scale_rows(plane, scales):
+            for q in range(4):
+                nc.sync.dma_start(
+                    out=plane[32 * q : 32 * q + 4, :, :].bitcast(I32),
+                    in_=scales[:, 4 * q : 4 * q + 4, :].rearrange("a r c -> r a c").bitcast(I32),
+                )
+
+        def quantise(op, rounded, width):
+            name = "%s%d%d%d" % (op[0], op[1], op[2], op[3] if len(op) > 3 else 0)
+            codes = keep.tile([P, width], U32, name=name + "_codes", align_bytes=64)
+            plane = keep.tile([P, width], U8, name=name + "_plane", align_bytes=64)
+            nc.vector.quantize_mx(out=codes[:].bitcast(FP8X4), scales=plane[:], in_=rounded[:, 0 : PACK * width])
+            tiles[op] = (codes, plane)
+
+        nc.vector.memset(w2_sraw[:].bitcast(U32), 0)
+        nc.vector.memset(w3_plane[:].bitcast(U32), 0)
+        for op in ORDER:
+            k = op[0]
+            if op == ("ld", "offs"):
+                nc.sync.dma_start(offsets[:], offs)
+            elif op == ("ld", "w2s"):
+                load_scale_rows(w2_sraw, w2_scales)
+            elif op == ("ld", "w2"):
+                nc.sync.dma_start(out=w2_raw[:].bitcast(I32), in_=w2_words.rearrange("a p c -> p a c").bitcast(I32))
+            elif op == ("ld", "w3"):
+                nc.sync.dma_start(out=w3_codes[:].bitcast(I32), in_=w3_words.rearrange("a p n t -> p a (n t)").bitcast(I32))
+            elif k == "ld" and op[1] == "wgt":
+                nc.sync.dma_start(out=wgt_sb[op[2]][:], in_=wgt[:, W * op[2] : W * (op[2] + 1)])
+            elif k == "ld" and op[1] == "win":
+                tiles[op] = windows.tile([P, T], F32, name="window")
+                nc.sync.dma_start(out=tiles[op][:], in_=xT_planes[op[2], op[3]])
+                if op[2:] == (0, 3):
+                    nc.sync.dma_start(out=b1_sb[:], in_=b1.rearrange("(b p t) -> p b t", p=P, t=PACK))
+                    nc.sync.dma_start(out=b2_sb[:], in_=b2.rearrange("(b p t) -> p b t", p=P, t=PACK))
+                    with nc.allow_non_contiguous_dma(reason="one bias value a partition"):
+                        nc.sync.dma_start(out=b3_sb[:], in_=b3.rearrange("(c p) -> p c", p=P))
+                    load_scale_rows(w3_plane, w3_scales)
+            elif k == "ld":
+                a, b = op[2:]
+                tiles[op] = ring4.tile([P, PACK, W], F32, name="w1_raw")
+                nc.sync.dma_start(out=tiles[op][:], in_=w1_rows[a, :, :, W * b : W * (b + 1)])
+            elif op == ("perm", "w2"):
+                nc.vector.tensor_copy(
+                    out=w2_codes[:].bitcast(U16).rearrange("p (g t m) -> p g t m", t=PACK, m=P),
+                    in_=w2_raw[:].rearrange("p a c -> p (a c)").bitcast(U16).rearrange("p (g m t) -> p g t m", t=PACK, m=P),
+                )
+            elif op == ("perm", "w2s"):
+                nc.vector.tensor_copy(
+                    out=w2_plane[:].rearrange("p (g t m) -> p g t m", t=PACK, m=P),
+                    in_=w2_sraw[:].rearrange("p a (b m t) -> p (a b) t m", t=PACK, m=P),
+                )
+            elif k == "g":
+                a, i, s = op[1:]
+                if ("picked", a, s) not in tiles:
+                    tiles[("picked", a, s)] = ring4.tile([P, PACK, W], F32, name="picked")
+                nc.vector.tensor_tensor(
+                    tiles[("picked", a, s)][:, i, :],
+                    tiles[("ld", "win", a, i)][:].indirect(offsets[:, 32 * s : 32 * (s + 1)]),
+                    wgt_sb[s][:],
+                    MULT,
+                )
+            elif k == "ix":
+                a, s, h = op[1:]
+                if h == 0:
+                    tiles[op[:3]] = ring2.tile([P, PACK * W], BF16, name="x_rounded", align_bytes=64)
+                copy_on(
+                    ASG[op],
+                    tiles[op[:3]][:, 1024 * h : 1024 * (h + 1)].rearrange("p (c i t) -> p c t i", i=4, t=PACK),
+                    tiles[("picked", a, s)][:, :, 256 * h : 256 * (h + 1)].rearrange("p t (c i) -> p c t i", i=4),
+                )
+            elif k == "iw":
+                a, b, h = op[1:]
+                if h == 0:
+                    tiles[op[:3]] = ring2.tile([P, PACK * W], BF16, name="w1_rounded", align_bytes=64)
+                copy_on(
+                    ASG[op],
+                    tiles[op[:3]][:].rearrange("p (t m j) -> p m j t", t=PACK, j=PACK)[:, 64 * h : 64 * (h + 1), :, :],
+                    tiles[("ld", "w1raw", a, b)][:, :, 256 * h : 256 * (h + 1)].rearrange("p j (m t) -> p m j t", t=PACK),
+                )
+            elif k == "ih":
+                b, s, q, h = op[1:]
+                half = W // NCH[(b, s)] // 2
+                if h == 0:
+                    tiles[op[:4]] = ring2.tile([P, PACK * W], BF16, name="h_rounded", align_bytes=64)
+                copy_on(
+                    ASG[op],
+                    tiles[op[:4]][:, PACK * half * h : PACK * half * (h + 1)].rearrange("p (c i t) -> p c t i", i=4, t=PACK),
+                    tiles[("mx", b, s, q)][:, :, half * h : half * (h + 1)].rearrange("p t (c i) -> p c t i", i=4),
+                )
+            elif k == "qx":
+                quantise(op, tiles[("ix",) + op[1:]], W)
+            elif k == "qw":
+                quantise(op, tiles[("iw",) + op[1:]], W)
+            elif k == "qh":
+                quantise(op, tiles[("ih",) + op[1:]], W // NCH[op[1:3]])
+            elif k == "c2":
+                b, s = op[1:]
+                sums = ring3.tile([P, PACK, W], F32, name="c2")
+                tiles[op] = sums
+                for t in range(PACK):
+                    acc = psum.tile([P, W], F32, name="acc")
+                    for a in range(2):
+                        col = H * a + W * b + P * t
+                        nc.tensor.matmul_mx(
+                            out=acc[:],
+                            lhsT=w2_codes[:, 2 * col : 2 * (col + P)].bitcast(FP4X4),
+                            lhsT_scale=w2_plane[:, col : col + P],
+                            rhs=tiles[("qx", a, s)][0][:].bitcast(FP8X4),
+                            rhs_scale=tiles[("qx", a, s)][1][:],
+                            start=(a == 0),
+                            stop=(a == 1),
+                        )
+                    add_bias(ASG[op + (t,)], sums[:, t, :], acc[:], b2_sb[:, b, t : t + 1])
+            elif k == "mx":
+                b, s, q = op[1:]
+                width = W // NCH[(b, s)]
+                cols = slice(width * q, width * (q + 1))
+                larger = ring2.tile([P, PACK, W], BF16, name="larger")
+                tiles[op] = larger
+                for t in range(PACK):
+                    acc = psum.tile([P, W], F32, name="acc")
+                    for a in range(2):
+                        nc.tensor.matmul_mx(
+                            out=acc[:, 0:width],
+                            lhsT=tiles[("qw", a, b)][0][:, P * t : P * (t + 1)].bitcast(FP8X4),
+                            lhsT_scale=tiles[("qw", a, b)][1][:, P * t : P * (t + 1)],
+                            rhs=tiles[("qx", a, s)][0][:, cols].bitcast(FP8X4),
+                            rhs_scale=tiles[("qx", a, s)][1][:, cols],
+                            start=(a == 0),
+                            stop=(a == 1),
+                        )
+                    nc.vector.scalar_tensor_tensor(
+                        out=larger[:, t, 0:width], in0=acc[:, 0:width], scalar=b1_sb[:, b, t : t + 1],
+                        in1=tiles[("c2", b, s)][:, t, cols], op0=ADD, op1=MAX
+                    )
+            elif k == "val":
+                s, q = op[1:]
+                n = max(NCH[(0, s)], NCH[(1, s)])
+                width = W // n
+                for c in range(2):
+                    acc = psum.tile([P, W], F32, name="acc")
+                    for b in range(2):
+                        nb = NCH[(b, s)]
+                        codes, plane = tiles[("qh", b, s, q * nb // n)]
+                        lo = width * q if nb < n else 0
+                        nc.tensor.matmul_mx(
+                            out=acc[:, 0:width],
+                            lhsT=w3_codes[:, b, P * c : P * (c + 1)].bitcast(FP8X4),
+                            lhsT_scale=w3_plane[:, b, P * c : P * (c + 1)],
+                            rhs=codes[:, lo : lo + width].bitcast(FP8X4),
+                            rhs_scale=plane[:, lo : lo + width],
+                            start=(b == 0),
+                            stop=(b == 1),
+                        )
+                    result = ring4.tile([P, W], F32, name="result")
+                    add_bias(ASG[op + (c,)], result[:, 0:width], acc[:, 0:width], b3_sb[:, c : c + 1])
+                    nc.sync.dma_start(
+                        out=out[P * c : P * (c + 1), W * s + width * q : W * s + width * (q + 1)], in_=result[:, 0:width]
+                    )

@@ -49,8 +49,8 @@ def tile_list_replay_maxout_values_kernel(
         b3_sb = keep.tile([P, 2], F32, name="b3_sb")
 
         NCH = {(0, 0): 1, (0, 1): 1, (1, 0): 1, (1, 1): 2}
-        ORDER = [('ld', 'offs'), ('ld', 'w2s'), ('ld', 'w2'), ('ld', 'wgt', 0), ('ld', 'win', 0, 0), ('g', 0, 0, 0), ('ld', 'wgt', 1), ('ld', 'win', 0, 1), ('ld', 'win', 0, 2), ('ld', 'win', 0, 3), ('ld', 'win', 1, 0), ('g', 0, 1, 0), ('ld', 'win', 1, 1), ('g', 1, 0, 1), ('perm', 'w2'), ('g', 0, 0, 1), ('ld', 'win', 1, 2),  ('g', 0, 2, 0), ('g', 0, 1, 1), ('ld', 'win', 1, 3), ('ld', 'w1raw', 0, 0), ('iw', 0, 0, 0), ('g', 1, 1, 1), ('g', 0, 2, 1), ('ld', 'w1raw', 1, 0), ('ld', 'w3'), ('g', 0, 3, 0), ('g', 1, 2, 1), ('g', 1, 3, 1), ('ix', 0, 0, 0), ('iw', 1, 0, 0), ('g', 1, 0, 0), ('perm', 'w2s'), ('ix', 0, 0, 1), ('qx', 0, 0), ('g', 0, 3, 1), ('iw', 0, 0, 1), ('ld', 'w1raw', 0, 1), ('g', 1, 1, 0), ('qw', 0, 0), ('ix', 1, 1, 0), ('ix', 1, 1, 1), ('iw', 1, 0, 1), ('ix', 0, 1, 0), ('ld', 'w1raw', 1, 1), ('g', 1, 2, 0), ('ix', 0, 1, 1), ('qx', 1, 1), ('qx', 0, 1), ('g', 1, 3, 0), ('iw', 1, 1, 0), ('iw', 0, 1, 0), ('qw', 1, 0), ('ix', 1, 0, 0), ('c2', 0, 1), ('ix', 1, 0, 1), ('iw', 1, 1, 1), ('qx', 1, 0), ('qw', 1, 1), ('c2', 0, 0), ('mx', 0, 1, 0), ('mx', 0, 0, 0), ('ih', 0, 1, 0, 0), ('iw', 0, 1, 1), ('ih', 0, 1, 0, 1), ('c2', 1, 0), ('ih', 0, 0, 0, 0), ('qw', 0, 1), ('ih', 0, 0, 0, 1), ('mx', 1, 0, 0), ('ih', 1, 0, 0, 0), ('c2', 1, 1), ('mx', 1, 1, 0), ('ih', 1, 0, 0, 1), ('ih', 1, 1, 0, 0), ('qh', 1, 0, 0), ('mx', 1, 1, 1), ('ih', 1, 1, 1, 0), ('qh', 0, 1, 0), ('ih', 1, 1, 0, 1), ('qh', 1, 1, 0), ('qh', 0, 0, 0), ('ih', 1, 1, 1, 1), ('qh', 1, 1, 1), ('val', 0, 0), ('val', 1, 0), ('val', 1, 1)]
-        ASG = {('ix', 0, 0, 0): 'S', ('iw', 0, 0, 0): 'S', ('ih', 0, 0, 0, 0): 'V', ('ix', 0, 0, 1): 'S', ('iw', 0, 0, 1): 'S', ('ih', 0, 0, 0, 1): 'S', ('c2', 0, 0, 0): 'S', ('c2', 0, 0, 1): 'S', ('c2', 0, 0, 2): 'V', ('c2', 0, 0, 3): 'S', ('val', 0, 0, 0): 'S', ('ix', 0, 1, 0): 'S', ('iw', 0, 1, 0): 'S', ('ih', 0, 1, 0, 0): 'S', ('ix', 0, 1, 1): 'S', ('iw', 0, 1, 1): 'S', ('ih', 0, 1, 0, 1): 'S', ('c2', 0, 1, 0): 'S', ('c2', 0, 1, 1): 'S', ('c2', 0, 1, 2): 'S', ('c2', 0, 1, 3): 'S', ('val', 0, 0, 1): 'V', ('ix', 1, 0, 0): 'V', ('iw', 1, 0, 0): 'V', ('ih', 1, 0, 0, 0): 'V', ('ix', 1, 0, 1): 'V', ('iw', 1, 0, 1): 'S', ('ih', 1, 0, 0, 1): 'S', ('c2', 1, 0, 0): 'S', ('c2', 1, 0, 1): 'S', ('c2', 1, 0, 2): 'S', ('c2', 1, 0, 3): 'S', ('val', 1, 0, 0): 'S', ('val', 1, 1, 0): 'V', ('ix', 1, 1, 0): 'V', ('iw', 1, 1, 0): 'S', ('ih', 1, 1, 0, 0): 'S', ('ih', 1, 1, 1, 0): 'V', ('ix', 1, 1, 1): 'S', ('iw', 1, 1, 1): 'V', ('ih', 1, 1, 0, 1): 'S', ('ih', 1, 1, 1, 1): 'S', ('c2', 1, 1, 0): 'S', ('c2', 1, 1, 1): 'S', ('c2', 1, 1, 2): 'V', ('c2', 1, 1, 3): 'S', ('val', 1, 0, 1): 'V', ('val', 1, 1, 1): 'S'}
+        ORDER = [('ld', 'offs'), ('ld', 'w2s'), ('ld', 'w2'), ('ld', 'wgt', 0), ('ld', 'win', 0, 0), ('perm', 'w2'), ('ld', 'wgt', 1), ('ld', 'win', 0, 1), ('ld', 'win', 0, 2), ('perm', 'w2s'), ('ld', 'win', 0, 3), ('g', 0, 0, 0), ('g', 0, 0, 1), ('g', 0, 1, 0), ('g', 0, 1, 1), ('ld', 'win', 1, 0), ('g', 0, 2, 0), ('g', 0, 2, 1), ('g', 0, 3, 0), ('ld', 'win', 1, 1), ('ld', 'w1raw', 0, 0), ('ix', 0, 0, 0), ('g', 0, 3, 1), ('g', 1, 0, 1), ('g', 1, 1, 1), ('ix', 0, 1, 1), ('ix', 0, 0, 1), ('ld', 'win', 1, 2), ('g', 1, 0, 0), ('ix', 0, 1, 0), ('g', 1, 1, 0), ('qx', 0, 0), ('g', 1, 2, 0), ('iw', 0, 0, 1), ('ld', 'win', 1, 3), ('iw', 0, 0, 0), ('g', 1, 2, 1), ('g', 1, 3, 0), ('ld', 'w1raw', 1, 0), ('g', 1, 3, 1), ('qx', 0, 1), ('ix', 1, 0, 0), ('ld', 'w1raw', 0, 1), ('ix', 1, 0, 1), ('ld', 'w1raw', 1, 1), ('qx', 1, 0), ('qw', 0, 0), ('iw', 1, 0, 0), ('iw', 1, 0, 1), ('ix', 1, 1, 1), ('ix', 1, 1, 0), ('qw', 1, 0), ('qx', 1, 1), ('c2', 0, 0, 3), ('c2', 0, 0, 2), ('c2', 0, 0, 0), ('iw', 1, 1, 0), ('c2', 0, 0, 1), ('iw', 0, 1, 0), ('mx', 0, 0, 0, 1), ('iw', 0, 1, 1), ('mx', 0, 0, 0, 3), ('mx', 0, 0, 0, 2), ('iw', 1, 1, 1), ('mx', 0, 0, 0, 0), ('qw', 0, 1), ('c2', 0, 1, 0), ('qw', 1, 1), ('ih', 0, 0, 0, 1), ('c2', 0, 1, 1), ('c2', 0, 1, 2), ('c2', 0, 1, 3), ('ld', 'w3'), ('mx', 0, 1, 0, 2), ('mx', 0, 1, 0, 0), ('c2', 1, 1, 2), ('ih', 0, 0, 0, 0), ('qh', 0, 0, 0), ('c2', 1, 0, 1), ('mx', 0, 1, 0, 1), ('mx', 0, 1, 0, 3), ('c2', 1, 0, 3), ('c2', 1, 0, 0), ('mx', 1, 0, 0, 0), ('mx', 1, 0, 0, 3), ('c2', 1, 1, 1), ('c2', 1, 0, 2), ('mx', 1, 0, 0, 2), ('mx', 1, 0, 0, 1), ('ih', 0, 1, 0, 0), ('ih', 0, 1, 0, 1), ('c2', 1, 1, 0), ('ih', 1, 0, 0, 1), ('ih', 1, 0, 0, 0), ('mx', 1, 1, 1, 0), ('qh', 0, 1, 0), ('mx', 1, 1, 1, 1), ('mx', 1, 1, 0, 2), ('mx', 1, 1, 1, 2), ('c2', 1, 1, 3), ('mx', 1, 1, 1, 3), ('mx', 1, 1, 0, 0), ('mx', 1, 1, 0, 1), ('mx', 1, 1, 0, 3), ('qh', 1, 0, 0), ('ih', 1, 1, 1, 0), ('ih', 1, 1, 1, 1), ('val', 0, 0, 0), ('ih', 1, 1, 0, 0), ('val', 0, 0, 1), ('ih', 1, 1, 0, 1), ('qh', 1, 1, 1), ('qh', 1, 1, 0), ('val', 1, 1, 1), ('val', 1, 1, 0), ('val', 1, 0, 1), ('val', 1, 0, 0)]
+        ASG = {('ix', 0, 0, 0): 'S', ('ix', 0, 0, 1): 'S', ('ix', 0, 1, 0): 'S', ('ix', 0, 1, 1): 'S', ('iw', 0, 0, 0): 'S', ('iw', 0, 0, 1): 'S', ('ix', 1, 0, 0): 'V', ('ix', 1, 0, 1): 'S', ('iw', 1, 0, 0): 'S', ('iw', 1, 0, 1): 'S', ('ix', 1, 1, 0): 'V', ('ix', 1, 1, 1): 'S', ('mode', 0, 0, 0): 'A', ('iw', 0, 1, 0): 'S', ('iw', 0, 1, 1): 'S', ('ih', 0, 0, 0, 0): 'S', ('ih', 0, 0, 0, 1): 'V', ('iw', 1, 1, 0): 'V', ('iw', 1, 1, 1): 'V', ('mode', 0, 1, 0): 'A', ('ih', 0, 1, 0, 0): 'V', ('ih', 0, 1, 0, 1): 'S', ('mode', 1, 0, 0): 'A', ('ih', 1, 0, 0, 0): 'S', ('ih', 1, 0, 0, 1): 'V', ('mode', 1, 1, 0): 'C', ('ih', 1, 1, 0, 0): 'S', ('ih', 1, 1, 0, 1): 'V', ('mode', 1, 1, 1): 'A', ('ih', 1, 1, 1, 0): 'S', ('ih', 1, 1, 1, 1): 'S', ('c2', 0, 0, 0): 'V', ('c2', 0, 0, 1): 'S', ('c2', 0, 0, 2): 'S', ('c2', 0, 0, 3): 'S', ('mx', 0, 0, 0, 0): 'V', ('mx', 0, 0, 0, 1): 'V', ('mx', 0, 0, 0, 2): 'V', ('mx', 0, 0, 0, 3): 'V', ('c2', 0, 1, 0): 'S', ('c2', 0, 1, 1): 'S', ('c2', 0, 1, 2): 'S', ('c2', 0, 1, 3): 'S', ('mx', 0, 1, 0, 0): 'S', ('mx', 0, 1, 0, 1): 'S', ('mx', 0, 1, 0, 2): 'S', ('mx', 0, 1, 0, 3): 'S', ('c2', 1, 0, 0): 'S', ('c2', 1, 0, 1): 'S', ('c2', 1, 0, 2): 'S', ('c2', 1, 0, 3): 'S', ('mx', 1, 0, 0, 0): 'V', ('mx', 1, 0, 0, 1): 'S', ('mx', 1, 0, 0, 2): 'V', ('mx', 1, 0, 0, 3): 'V', ('c2', 1, 1, 0): 'S', ('c2', 1, 1, 1): 'S', ('c2', 1, 1, 2): 'S', ('c2', 1, 1, 3): 'S', ('mx', 1, 1, 0, 0): 'S', ('mx', 1, 1, 0, 1): 'S', ('mx', 1, 1, 0, 2): 'S', ('mx', 1, 1, 0, 3): 'S', ('val', 0, 0, 0): 'S', ('val', 0, 0, 1): 'S', ('mx', 1, 1, 1, 0): 'S', ('mx', 1, 1, 1, 1): 'S', ('mx', 1, 1, 1, 2): 'S', ('mx', 1, 1, 1, 3): 'S', ('val', 1, 0, 0): 'V', ('val', 1, 0, 1): 'V', ('val', 1, 1, 0): 'S', ('val', 1, 1, 1): 'V'}
         xT_planes = xT.rearrange("(a p i) t -> a i p t", p=P, i=PACK)
         w1_rows = w1.rearrange("(a p j) c -> a p j c", p=P, j=PACK)
         tiles = {}
@@ -95,17 +95,19 @@ def tile_list_replay_maxout_values_kernel(
                 nc.sync.dma_start(out=w2_raw[:].bitcast(I32), in_=w2_words.rearrange("a p c -> p a c").bitcast(I32))
             elif op == ("ld", "w3"):
                 nc.sync.dma_start(out=w3_codes[:].bitcast(I32), in_=w3_words.rearrange("a p n t -> p a (n t)").bitcast(I32))
+                load_scale_rows(w3_plane, w3_scales)
             elif k == "ld" and op[1] == "wgt":
                 nc.sync.dma_start(out=wgt_sb[op[2]][:], in_=wgt[:, W * op[2] : W * (op[2] + 1)])
             elif k == "ld" and op[1] == "win":
                 tiles[op] = windows.tile([P, T], F32, name="window")
                 nc.sync.dma_start(out=tiles[op][:], in_=xT_planes[op[2], op[3]])
-                if op[2:] == (0, 3):
-                    nc.sync.dma_start(out=b1_sb[:], in_=b1.rearrange("(b p t) -> p b t", p=P, t=PACK))
+                if op[2:] == (0, 1):
                     nc.sync.dma_start(out=b2_sb[:], in_=b2.rearrange("(b p t) -> p b t", p=P, t=PACK))
+                if op[2:] == (0, 2):
+                    nc.sync.dma_start(out=b1_sb[:], in_=b1.rearrange("(b p t) -> p b t", p=P, t=PACK))
+                if op[2:] == (0, 3):
                     with nc.allow_non_contiguous_dma(reason="one bias value a partition"):
                         nc.sync.dma_start(out=b3_sb[:], in_=b3.rearrange("(c p) -> p c", p=P))
-                    load_scale_rows(w3_plane, w3_scales)
             elif k == "ld":
                 a, b = op[2:]
                 tiles[op] = ring4.tile([P, PACK, W], F32, name="w1_raw")
@@ -132,7 +134,7 @@ def tile_list_replay_maxout_values_kernel(
                 )
             elif k == "ix":
                 a, s, h = op[1:]
-                if h == 0:
+                if op[:3] not in tiles:
                     tiles[op[:3]] = ring2.tile([P, PACK * W], BF16, name="x_rounded", align_bytes=64)
                 copy_on(
                     ASG[op],
@@ -141,7 +143,7 @@ def tile_list_replay_maxout_values_kernel(
                 )
             elif k == "iw":
                 a, b, h = op[1:]
-                if h == 0:
+                if op[:3] not in tiles:
                     tiles[op[:3]] = ring2.tile([P, PACK * W], BF16, name="w1_rounded", align_bytes=64)
                 copy_on(
                     ASG[op],
@@ -151,8 +153,17 @@ def tile_list_replay_maxout_values_kernel(
             elif k == "ih":
                 b, s, q, h = op[1:]
                 half = W // NCH[(b, s)] // 2
-                if h == 0:
+                if op[:4] not in tiles:
                     tiles[op[:4]] = ring2.tile([P, PACK * W], BF16, name="h_rounded", align_bytes=64)
+                if ASG[("mode",) + op[1:4]] == "C":
+                    lo = 2 * half * q + half * h
+                    nc.vector.tensor_tensor(
+                        tiles[op[:4]][:, PACK * half * h : PACK * half * (h + 1)].rearrange("p (c i t) -> p c t i", i=2, t=PACK),
+                        tiles[("mx", b, s, q)][:, :, half * h : half * (h + 1)].rearrange("p t (c i) -> p c t i", i=2),
+                        tiles[("c2", b, s)][:, :, lo : lo + half].rearrange("p t (c i) -> p c t i", i=2),
+                        MAX,
+                    )
+                    continue
                 copy_on(
                     ASG[op],
                     tiles[op[:4]][:, PACK * half * h : PACK * half * (h + 1)].rearrange("p (c i t) -> p c t i", i=4, t=PACK),
@@ -165,10 +176,11 @@ def tile_list_replay_maxout_values_kernel(
             elif k == "qh":
                 quantise(op, tiles[("ih",) + op[1:]], W // NCH[op[1:3]])
             elif k == "c2":
-                b, s = op[1:]
-                sums = ring3.tile([P, PACK, W], F32, name="c2")
-                tiles[op] = sums
-                for t in range(PACK):
+                b, s = op[1:3]
+                if op[:3] not in tiles:
+                    tiles[op[:3]] = ring3.tile([P, PACK, W], F32, name="c2")
+                sums = tiles[op[:3]]
+                for t in op[3:]:
                     acc = psum.tile([P, W], F32, name="acc")
                     for a in range(2):
                         col = H * a + W * b + P * t
@@ -181,14 +193,18 @@ def tile_list_replay_maxout_values_kernel(
                             start=(a == 0),
                             stop=(a == 1),
                         )
-                    add_bias(ASG[op + (t,)], sums[:, t, :], acc[:], b2_sb[:, b, t : t + 1])
+                    add_bias(ASG[op], sums[:, t, :], acc[:], b2_sb[:, b, t : t + 1])
             elif k == "mx":
-                b, s, q = op[1:]
+                b, s, q = op[1:4]
                 width = W // NCH[(b, s)]
                 cols = slice(width * q, width * (q + 1))
-                larger = ring2.tile([P, PACK, W], BF16, name="larger")
-                tiles[op] = larger
-                for t in range(PACK):
+                if op[:4] not in tiles:
+                    if ASG[("mode",) + op[1:4]] == "A":
+                        tiles[op[:4]] = ring2.tile([P, PACK, W], BF16, name="larger")
+                    else:
+                        tiles[op[:4]] = ring2.tile([P, PACK, width], F32, name="c1")
+                larger = tiles[op[:4]]
+                for t in op[4:]:
                     acc = psum.tile([P, W], F32, name="acc")
                     for a in range(2):
                         nc.tensor.matmul_mx(
@@ -200,15 +216,18 @@ def tile_list_replay_maxout_values_kernel(
                             start=(a == 0),
                             stop=(a == 1),
                         )
+                    if ASG[("mode",) + op[1:4]] == "C":
+                        add_bias(ASG[op], larger[:, t, :], acc[:, 0:width], b1_sb[:, b, t : t + 1])
+                        continue
                     nc.vector.scalar_tensor_tensor(
                         out=larger[:, t, 0:width], in0=acc[:, 0:width], scalar=b1_sb[:, b, t : t + 1],
                         in1=tiles[("c2", b, s)][:, t, cols], op0=ADD, op1=MAX
                     )
             elif k == "val":
-                s, q = op[1:]
+                s, q = op[1:3]
                 n = max(NCH[(0, s)], NCH[(1, s)])
                 width = W // n
-                for c in range(2):
+                for c in op[3:]:
                     acc = psum.tile([P, W], F32, name="acc")
                     for b in range(2):
                         nb = NCH[(b, s)]
@@ -224,7 +243,7 @@ def tile_list_replay_maxout_values_kernel(
                             stop=(b == 1),
                         )
                     result = ring4.tile([P, W], F32, name="result")
-                    add_bias(ASG[op + (c,)], result[:, 0:width], acc[:, 0:width], b3_sb[:, c : c + 1])
+                    add_bias(ASG[op], result[:, 0:width], acc[:, 0:width], b3_sb[:, c : c + 1])
                     nc.sync.dma_start(
                         out=out[P * c : P * (c + 1), W * s + width * q : W * s + width * (q + 1)], in_=result[:, 0:width]
                     )

@@ -48,9 +48,9 @@ def tile_list_replay_maxout_values_kernel(
         b2_sb = keep.tile([P, 2, PACK], F32, name="b2_sb")
         b3_sb = keep.tile([P, 2], F32, name="b3_sb")
 
-        NCH = {(0, 0): 1, (0, 1): 1, (1, 0): 1, (1, 1): 2}
-        ORDER = [('ld', 'offs'), ('ld', 'w2s'), ('ld', 'w2'), ('ld', 'wgt', 0), ('ld', 'win', 0, 0), ('perm', 'w2'), ('ld', 'wgt', 1), ('ld', 'win', 0, 1), ('ld', 'win', 0, 2), ('perm', 'w2s'), ('ld', 'win', 0, 3), ('g', 0, 0, 0), ('g', 0, 0, 1), ('g', 0, 1, 0), ('g', 0, 1, 1), ('ld', 'win', 1, 0), ('g', 0, 2, 0), ('g', 0, 2, 1), ('g', 0, 3, 0), ('ld', 'win', 1, 1), ('ld', 'w1raw', 0, 0), ('ix', 0, 0, 0), ('g', 0, 3, 1), ('g', 1, 0, 1), ('g', 1, 1, 1), ('ix', 0, 1, 1), ('ix', 0, 0, 1), ('ld', 'win', 1, 2), ('g', 1, 0, 0), ('ix', 0, 1, 0), ('g', 1, 1, 0), ('qx', 0, 0), ('g', 1, 2, 0), ('iw', 0, 0, 1), ('ld', 'win', 1, 3), ('iw', 0, 0, 0), ('g', 1, 2, 1), ('g', 1, 3, 0), ('ld', 'w1raw', 1, 0), ('g', 1, 3, 1), ('qx', 0, 1), ('ix', 1, 0, 0), ('ld', 'w1raw', 0, 1), ('ix', 1, 0, 1), ('ld', 'w1raw', 1, 1), ('qx', 1, 0), ('qw', 0, 0), ('iw', 1, 0, 0), ('iw', 1, 0, 1), ('ix', 1, 1, 1), ('ix', 1, 1, 0), ('qw', 1, 0), ('qx', 1, 1), ('c2', 0, 0, 3), ('c2', 0, 0, 2), ('c2', 0, 0, 0), ('iw', 1, 1, 0), ('c2', 0, 0, 1), ('iw', 0, 1, 0), ('mx', 0, 0, 0, 1), ('iw', 0, 1, 1), ('mx', 0, 0, 0, 3), ('mx', 0, 0, 0, 2), ('iw', 1, 1, 1), ('mx', 0, 0, 0, 0), ('qw', 0, 1), ('c2', 0, 1, 0), ('qw', 1, 1), ('ih', 0, 0, 0, 1), ('c2', 0, 1, 1), ('c2', 0, 1, 2), ('c2', 0, 1, 3), ('ld', 'w3'), ('mx', 0, 1, 0, 2), ('mx', 0, 1, 0, 0), ('c2', 1, 1, 2), ('ih', 0, 0, 0, 0), ('qh', 0, 0, 0), ('c2', 1, 0, 1), ('mx', 0, 1, 0, 1), ('mx', 0, 1, 0, 3), ('c2', 1, 0, 3), ('c2', 1, 0, 0), ('mx', 1, 0, 0, 0), ('mx', 1, 0, 0, 3), ('c2', 1, 1, 1), ('c2', 1, 0, 2), ('mx', 1, 0, 0, 2), ('mx', 1, 0, 0, 1), ('ih', 0, 1, 0, 0), ('ih', 0, 1, 0, 1), ('c2', 1, 1, 0), ('ih', 1, 0, 0, 1), ('ih', 1, 0, 0, 0), ('mx', 1, 1, 1, 0), ('qh', 0, 1, 0), ('mx', 1, 1, 1, 1), ('mx', 1, 1, 0, 2), ('mx', 1, 1, 1, 2), ('c2', 1, 1, 3), ('mx', 1, 1, 1, 3), ('mx', 1, 1, 0, 0), ('mx', 1, 1, 0, 1), ('mx', 1, 1, 0, 3), ('qh', 1, 0, 0), ('ih', 1, 1, 1, 0), ('ih', 1, 1, 1, 1), ('val', 0, 0, 0), ('ih', 1, 1, 0, 0), ('val', 0, 0, 1), ('ih', 1, 1, 0, 1), ('qh', 1, 1, 1), ('qh', 1, 1, 0), ('val', 1, 1, 1), ('val', 1, 1, 0), ('val', 1, 0, 1), ('val', 1, 0, 0)]
-        ASG = {('ix', 0, 0, 0): 'S', ('ix', 0, 0, 1): 'S', ('ix', 0, 1, 0): 'S', ('ix', 0, 1, 1): 'S', ('iw', 0, 0, 0): 'S', ('iw', 0, 0, 1): 'S', ('ix', 1, 0, 0): 'V', ('ix', 1, 0, 1): 'S', ('iw', 1, 0, 0): 'S', ('iw', 1, 0, 1): 'S', ('ix', 1, 1, 0): 'V', ('ix', 1, 1, 1): 'S', ('mode', 0, 0, 0): 'A', ('iw', 0, 1, 0): 'S', ('iw', 0, 1, 1): 'S', ('ih', 0, 0, 0, 0): 'S', ('ih', 0, 0, 0, 1): 'V', ('iw', 1, 1, 0): 'V', ('iw', 1, 1, 1): 'V', ('mode', 0, 1, 0): 'A', ('ih', 0, 1, 0, 0): 'V', ('ih', 0, 1, 0, 1): 'S', ('mode', 1, 0, 0): 'A', ('ih', 1, 0, 0, 0): 'S', ('ih', 1, 0, 0, 1): 'V', ('mode', 1, 1, 0): 'C', ('ih', 1, 1, 0, 0): 'S', ('ih', 1, 1, 0, 1): 'V', ('mode', 1, 1, 1): 'A', ('ih', 1, 1, 1, 0): 'S', ('ih', 1, 1, 1, 1): 'S', ('c2', 0, 0, 0): 'V', ('c2', 0, 0, 1): 'S', ('c2', 0, 0, 2): 'S', ('c2', 0, 0, 3): 'S', ('mx', 0, 0, 0, 0): 'V', ('mx', 0, 0, 0, 1): 'V', ('mx', 0, 0, 0, 2): 'V', ('mx', 0, 0, 0, 3): 'V', ('c2', 0, 1, 0): 'S', ('c2', 0, 1, 1): 'S', ('c2', 0, 1, 2): 'S', ('c2', 0, 1, 3): 'S', ('mx', 0, 1, 0, 0): 'S', ('mx', 0, 1, 0, 1): 'S', ('mx', 0, 1, 0, 2): 'S', ('mx', 0, 1, 0, 3): 'S', ('c2', 1, 0, 0): 'S', ('c2', 1, 0, 1): 'S', ('c2', 1, 0, 2): 'S', ('c2', 1, 0, 3): 'S', ('mx', 1, 0, 0, 0): 'V', ('mx', 1, 0, 0, 1): 'S', ('mx', 1, 0, 0, 2): 'V', ('mx', 1, 0, 0, 3): 'V', ('c2', 1, 1, 0): 'S', ('c2', 1, 1, 1): 'S', ('c2', 1, 1, 2): 'S', ('c2', 1, 1, 3): 'S', ('mx', 1, 1, 0, 0): 'S', ('mx', 1, 1, 0, 1): 'S', ('mx', 1, 1, 0, 2): 'S', ('mx', 1, 1, 0, 3): 'S', ('val', 0, 0, 0): 'S', ('val', 0, 0, 1): 'S', ('mx', 1, 1, 1, 0): 'S', ('mx', 1, 1, 1, 1): 'S', ('mx', 1, 1, 1, 2): 'S', ('mx', 1, 1, 1, 3): 'S', ('val', 1, 0, 0): 'V', ('val', 1, 0, 1): 'V', ('val', 1, 1, 0): 'S', ('val', 1, 1, 1): 'V'}
+        NCH = {(0, 0): 1, (0, 1): 2, (1, 0): 1, (1, 1): 2}
+        ORDER = [('ld', 'offs'), ('ld', 'w2s'), ('perm', 'w2s'), ('ld', 'w2'), ('ld', 'wgt', 0), ('perm', 'w2'), ('ld', 'win', 0, 0), ('ld', 'wgt', 1), ('ld', 'win', 0, 1), ('g', 0, 0, 0), ('g', 0, 0, 1), ('ld', 'win', 0, 2), ('ld', 'win', 0, 3), ('ld', 'win', 1, 0), ('g', 0, 1, 0), ('g', 0, 1, 1), ('g', 0, 2, 0), ('g', 0, 2, 1), ('g', 0, 3, 1), ('g', 0, 3, 0), ('ld', 'win', 1, 1), ('ld', 'w1raw', 0, 0), ('g', 1, 0, 1), ('g', 1, 0, 0), ('ix', 0, 1, 1), ('ix', 0, 1, 0), ('ld', 'win', 1, 2), ('ix', 0, 0, 0), ('ix', 0, 0, 1), ('ld', 'win', 1, 3), ('qx', 0, 1), ('iw', 0, 0, 0), ('iw', 0, 0, 1), ('g', 1, 1, 1), ('g', 1, 1, 0), ('qx', 0, 0), ('ld', 'w1raw', 1, 0), ('qw', 0, 0), ('g', 1, 2, 0), ('g', 1, 3, 0), ('g', 1, 3, 1), ('ix', 1, 0, 1), ('iw', 1, 0, 1), ('iw', 1, 0, 0), ('ix', 1, 0, 0), ('ld', 'w1raw', 0, 1), ('g', 1, 2, 1), ('qx', 1, 0), ('qw', 1, 0), ('iw', 0, 1, 0), ('iw', 0, 1, 1), ('ix', 1, 1, 1), ('ix', 1, 1, 0), ('ld', 'w1raw', 1, 1), ('iw', 1, 1, 1), ('iw', 1, 1, 0), ('c2', 0, 0, 3), ('c2', 0, 0, 1), ('c2', 0, 0, 0), ('c2', 0, 0, 2), ('mx', 0, 0, 0, 3), ('c2', 1, 0, 1), ('c2', 1, 0, 3), ('c2', 1, 0, 0), ('c2', 1, 0, 2), ('qx', 1, 1), ('qw', 1, 1), ('qw', 0, 1), ('mx', 0, 0, 0, 1), ('mx', 0, 0, 0, 0), ('mx', 0, 0, 0, 2), ('c2', 0, 1, 2), ('c2', 0, 1, 0), ('mx', 1, 0, 0, 3), ('mx', 1, 0, 0, 0), ('ih', 0, 0, 0, 0), ('ld', 'w3'), ('c2', 0, 1, 1), ('c2', 0, 1, 3), ('ih', 0, 0, 0, 1), ('mx', 1, 0, 0, 1), ('mx', 1, 0, 0, 2), ('qh', 0, 0, 0), ('c2', 1, 1, 3), ('c2', 1, 1, 1), ('ih', 1, 0, 0, 1), ('ih', 1, 0, 0, 0), ('mx', 0, 1, 0, 3), ('mx', 0, 1, 0, 1), ('mx', 0, 1, 0, 0), ('mx', 0, 1, 0, 2), ('c2', 1, 1, 2), ('c2', 1, 1, 0), ('qh', 1, 0, 0), ('mx', 1, 1, 0, 1), ('mx', 1, 1, 0, 0), ('mx', 1, 1, 0, 3), ('mx', 1, 1, 0, 2), ('ih', 0, 1, 0, 0), ('ih', 0, 1, 0, 1), ('mx', 0, 1, 1, 0), ('mx', 0, 1, 1, 2), ('mx', 0, 1, 1, 3), ('mx', 0, 1, 1, 1), ('qh', 0, 1, 0), ('ih', 1, 1, 0, 1), ('ih', 1, 1, 0, 0), ('mx', 1, 1, 1, 3), ('mx', 1, 1, 1, 2), ('mx', 1, 1, 1, 1), ('qh', 1, 1, 0), ('mx', 1, 1, 1, 0), ('ih', 0, 1, 1, 0), ('ih', 0, 1, 1, 1), ('val', 1, 0, 1), ('val', 0, 0, 0), ('val', 0, 0, 1), ('ih', 1, 1, 1, 1), ('ih', 1, 1, 1, 0), ('qh', 0, 1, 1), ('val', 1, 0, 0), ('qh', 1, 1, 1), ('val', 1, 1, 0), ('val', 1, 1, 1)]
+        ASG = {('ix', 0, 0, 0): 'S', ('ix', 0, 0, 1): 'S', ('ix', 0, 1, 0): 'S', ('ix', 0, 1, 1): 'S', ('iw', 0, 0, 0): 'S', ('iw', 0, 0, 1): 'S', ('ix', 1, 0, 0): 'V', ('ix', 1, 0, 1): 'S', ('iw', 1, 0, 0): 'S', ('iw', 1, 0, 1): 'S', ('iw', 0, 1, 0): 'V', ('iw', 0, 1, 1): 'V', ('mode', 0, 0, 0): 'A', ('iw', 1, 1, 0): 'V', ('iw', 1, 1, 1): 'V', ('ix', 1, 1, 0): 'S', ('ix', 1, 1, 1): 'S', ('ih', 0, 0, 0, 0): 'S', ('ih', 0, 0, 0, 1): 'V', ('mode', 1, 0, 0): 'A', ('ih', 1, 0, 0, 0): 'V', ('ih', 1, 0, 0, 1): 'S', ('mode', 0, 1, 0): 'A', ('ih', 0, 1, 0, 0): 'S', ('ih', 0, 1, 0, 1): 'S', ('mode', 1, 1, 0): 'A', ('ih', 1, 1, 0, 0): 'S', ('ih', 1, 1, 0, 1): 'S', ('mode', 0, 1, 1): 'A', ('ih', 0, 1, 1, 0): 'V', ('ih', 0, 1, 1, 1): 'S', ('mode', 1, 1, 1): 'C', ('ih', 1, 1, 1, 0): 'V', ('ih', 1, 1, 1, 1): 'V', ('c2', 0, 0, 0): 'S', ('c2', 0, 0, 1): 'S', ('c2', 0, 0, 2): 'S', ('c2', 0, 0, 3): 'S', ('c2', 1, 0, 0): 'S', ('c2', 1, 0, 1): 'S', ('c2', 1, 0, 2): 'S', ('c2', 1, 0, 3): 'S', ('mx', 0, 0, 0, 0): 'V', ('mx', 0, 0, 0, 1): 'V', ('mx', 0, 0, 0, 2): 'S', ('mx', 0, 0, 0, 3): 'V', ('mx', 1, 0, 0, 0): 'V', ('mx', 1, 0, 0, 1): 'S', ('mx', 1, 0, 0, 2): 'V', ('mx', 1, 0, 0, 3): 'S', ('c2', 0, 1, 0): 'S', ('c2', 0, 1, 1): 'S', ('c2', 0, 1, 2): 'S', ('c2', 0, 1, 3): 'S', ('c2', 1, 1, 0): 'S', ('c2', 1, 1, 1): 'S', ('c2', 1, 1, 2): 'S', ('c2', 1, 1, 3): 'S', ('mx', 0, 1, 0, 0): 'V', ('mx', 0, 1, 0, 1): 'V', ('mx', 0, 1, 0, 2): 'S', ('mx', 0, 1, 0, 3): 'S', ('mx', 1, 1, 0, 0): 'V', ('mx', 1, 1, 0, 1): 'S', ('mx', 1, 1, 0, 2): 'S', ('mx', 1, 1, 0, 3): 'V', ('val', 0, 0, 0): 'S', ('val', 0, 0, 1): 'S', ('mx', 0, 1, 1, 0): 'V', ('mx', 0, 1, 1, 1): 'V', ('mx', 0, 1, 1, 2): 'S', ('mx', 0, 1, 1, 3): 'V', ('mx', 1, 1, 1, 0): 'V', ('mx', 1, 1, 1, 1): 'S', ('mx', 1, 1, 1, 2): 'S', ('mx', 1, 1, 1, 3): 'S', ('val', 1, 0, 0): 'S', ('val', 1, 0, 1): 'S', ('val', 1, 1, 0): 'V', ('val', 1, 1, 1): 'S'}
         xT_planes = xT.rearrange("(a p i) t -> a i p t", p=P, i=PACK)
         w1_rows = w1.rearrange("(a p j) c -> a p j c", p=P, j=PACK)
         tiles = {}
@@ -242,7 +242,7 @@ def tile_list_replay_maxout_values_kernel(
                             start=(b == 0),
                             stop=(b == 1),
                         )
-                    result = ring4.tile([P, W], F32, name="result")
+                    result = keep.tile([P, W], F32, name="result%d%d%d" % op[1:])
                     add_bias(ASG[op], result[:, 0:width], acc[:, 0:width], b3_sb[:, c : c + 1])
                     nc.sync.dma_start(
                         out=out[P * c : P * (c + 1), W * s + width * q : W * s + width * (q + 1)], in_=result[:, 0:width]

@@ -16,31 +16,38 @@ FP4X4 = mybir.dt.float4_e2m1fn_x4
 MULT = mybir.AluOpType.mult
 ADD = mybir.AluOpType.add
 MAX = mybir.AluOpType.max
-IDENT = mybir.ActivationFunctionType.Identity
+IDENTITY = mybir.ActivationFunctionType.Identity
 
 P = 128
 PACK = 4
-PASS = P * PACK
-W = 512
+BANK = 512
+LIST_COLUMNS = BANK // 16
+RUN = 4
+
+SPAN_0, SPAN_1, SPAN_2 = (0, 512), (512, 256), (768, 256)
+
+WHOLE, LOWER, UPPER = (0, 2), (0, 1), (1, 2)
+ALL_T = range(PACK)
 
 
 def tile_list_replay_maxout_values_kernel(
     tc, xT, wgt, offs, w1, b1, w2_words, w2_scales, b2, w3_words, w3_scales, b3, out
 ):
     nc = tc.nc
+    vector, scalar = nc.vector, nc.scalar
     with ExitStack() as ctx:
         keep = ctx.enter_context(tc.tile_pool(name="keep", bufs=1))
         windows = ctx.enter_context(tc.tile_pool(name="windows", bufs=6))
-        ring3 = ctx.enter_context(tc.tile_pool(name="ring3", bufs=3))
-        ring2 = ctx.enter_context(tc.tile_pool(name="ring2", bufs=2))
-        ring4 = ctx.enter_context(tc.tile_pool(name="ring4", bufs=4))
+        critic2_sums = ctx.enter_context(tc.tile_pool(name="critic2_sums", bufs=3))
+        staging = ctx.enter_context(tc.tile_pool(name="staging", bufs=2))
+        quarters = ctx.enter_context(tc.tile_pool(name="quarters", bufs=4))
         psum = ctx.enter_context(tc.psum_pool(name="psum", bufs=8))
 
         offsets = keep.tile([P, S // 16], U16, name="offsets")
-        wgt_sb = [keep.tile([P, W], F32, name="wgt%d" % s) for s in range(2)]
-        w2_raw = keep.tile([P, 2, 2 * H], U8, name="w2_raw", align_bytes=64)
+        wgt_sb = [keep.tile([P, BANK], F32, name="wgt%d" % s) for s in range(2)]
+        w2_loaded = keep.tile([P, 2, 2 * H], U8, name="w2_loaded", align_bytes=64)
         w2_codes = keep.tile([P, 2 * 2 * H], U8, name="w2_codes", align_bytes=64)
-        w2_sraw = keep.tile([P, 2, H], U8, name="w2_sraw", align_bytes=64)
+        w2_plane_loaded = keep.tile([P, 2, H], U8, name="w2_plane_loaded", align_bytes=64)
         w2_plane = keep.tile([P, 2 * H], U8, name="w2_plane", align_bytes=64)
         w3_codes = keep.tile([P, 2, N], U32, name="w3_codes", align_bytes=64)
         w3_plane = keep.tile([P, 2, N], U8, name="w3_plane", align_bytes=64)
@@ -48,202 +55,268 @@ def tile_list_replay_maxout_values_kernel(
         b2_sb = keep.tile([P, 2, PACK], F32, name="b2_sb")
         b3_sb = keep.tile([P, 2], F32, name="b3_sb")
 
-        NCH = {(0, 0): 1, (0, 1): 2, (1, 0): 1, (1, 1): 2}
-        ORDER = [('ld', 'offs'), ('ld', 'w2s'), ('perm', 'w2s'), ('ld', 'w2'), ('ld', 'wgt', 0), ('perm', 'w2'), ('ld', 'win', 0, 0), ('ld', 'wgt', 1), ('ld', 'win', 0, 1), ('g', 0, 0, 0), ('g', 0, 0, 1), ('ld', 'win', 0, 2), ('ld', 'win', 0, 3), ('ld', 'win', 1, 0), ('g', 0, 1, 0), ('g', 0, 1, 1), ('g', 0, 2, 0), ('g', 0, 2, 1), ('g', 0, 3, 1), ('g', 0, 3, 0), ('ld', 'win', 1, 1), ('ld', 'w1raw', 0, 0), ('g', 1, 0, 1), ('g', 1, 0, 0), ('ix', 0, 1, 1), ('ix', 0, 1, 0), ('ld', 'win', 1, 2), ('ix', 0, 0, 0), ('ix', 0, 0, 1), ('ld', 'win', 1, 3), ('qx', 0, 1), ('iw', 0, 0, 0), ('iw', 0, 0, 1), ('g', 1, 1, 1), ('g', 1, 1, 0), ('qx', 0, 0), ('ld', 'w1raw', 1, 0), ('qw', 0, 0), ('g', 1, 2, 0), ('g', 1, 3, 0), ('g', 1, 3, 1), ('ix', 1, 0, 1), ('iw', 1, 0, 1), ('iw', 1, 0, 0), ('ix', 1, 0, 0), ('ld', 'w1raw', 0, 1), ('g', 1, 2, 1), ('qx', 1, 0), ('qw', 1, 0), ('iw', 0, 1, 0), ('iw', 0, 1, 1), ('ix', 1, 1, 1), ('ix', 1, 1, 0), ('ld', 'w1raw', 1, 1), ('iw', 1, 1, 1), ('iw', 1, 1, 0), ('c2', 0, 0, 3), ('c2', 0, 0, 1), ('c2', 0, 0, 0), ('c2', 0, 0, 2), ('mx', 0, 0, 0, 3), ('c2', 1, 0, 1), ('c2', 1, 0, 3), ('c2', 1, 0, 0), ('c2', 1, 0, 2), ('qx', 1, 1), ('qw', 1, 1), ('qw', 0, 1), ('mx', 0, 0, 0, 1), ('mx', 0, 0, 0, 0), ('mx', 0, 0, 0, 2), ('c2', 0, 1, 2), ('c2', 0, 1, 0), ('mx', 1, 0, 0, 3), ('mx', 1, 0, 0, 0), ('ih', 0, 0, 0, 0), ('ld', 'w3'), ('c2', 0, 1, 1), ('c2', 0, 1, 3), ('ih', 0, 0, 0, 1), ('mx', 1, 0, 0, 1), ('mx', 1, 0, 0, 2), ('qh', 0, 0, 0), ('c2', 1, 1, 3), ('c2', 1, 1, 1), ('ih', 1, 0, 0, 1), ('ih', 1, 0, 0, 0), ('mx', 0, 1, 0, 3), ('mx', 0, 1, 0, 1), ('mx', 0, 1, 0, 0), ('mx', 0, 1, 0, 2), ('c2', 1, 1, 2), ('c2', 1, 1, 0), ('qh', 1, 0, 0), ('mx', 1, 1, 0, 1), ('mx', 1, 1, 0, 0), ('mx', 1, 1, 0, 3), ('mx', 1, 1, 0, 2), ('ih', 0, 1, 0, 0), ('ih', 0, 1, 0, 1), ('mx', 0, 1, 1, 0), ('mx', 0, 1, 1, 2), ('mx', 0, 1, 1, 3), ('mx', 0, 1, 1, 1), ('qh', 0, 1, 0), ('ih', 1, 1, 0, 1), ('ih', 1, 1, 0, 0), ('mx', 1, 1, 1, 3), ('mx', 1, 1, 1, 2), ('mx', 1, 1, 1, 1), ('qh', 1, 1, 0), ('mx', 1, 1, 1, 0), ('ih', 0, 1, 1, 0), ('ih', 0, 1, 1, 1), ('val', 1, 0, 1), ('val', 0, 0, 0), ('val', 0, 0, 1), ('ih', 1, 1, 1, 1), ('ih', 1, 1, 1, 0), ('qh', 0, 1, 1), ('val', 1, 0, 0), ('qh', 1, 1, 1), ('val', 1, 1, 0), ('val', 1, 1, 1)]
-        ASG = {('ix', 0, 0, 0): 'S', ('ix', 0, 0, 1): 'S', ('ix', 0, 1, 0): 'S', ('ix', 0, 1, 1): 'S', ('iw', 0, 0, 0): 'S', ('iw', 0, 0, 1): 'S', ('ix', 1, 0, 0): 'V', ('ix', 1, 0, 1): 'S', ('iw', 1, 0, 0): 'S', ('iw', 1, 0, 1): 'S', ('iw', 0, 1, 0): 'V', ('iw', 0, 1, 1): 'V', ('mode', 0, 0, 0): 'A', ('iw', 1, 1, 0): 'V', ('iw', 1, 1, 1): 'V', ('ix', 1, 1, 0): 'S', ('ix', 1, 1, 1): 'S', ('ih', 0, 0, 0, 0): 'S', ('ih', 0, 0, 0, 1): 'V', ('mode', 1, 0, 0): 'A', ('ih', 1, 0, 0, 0): 'V', ('ih', 1, 0, 0, 1): 'S', ('mode', 0, 1, 0): 'A', ('ih', 0, 1, 0, 0): 'S', ('ih', 0, 1, 0, 1): 'S', ('mode', 1, 1, 0): 'A', ('ih', 1, 1, 0, 0): 'S', ('ih', 1, 1, 0, 1): 'S', ('mode', 0, 1, 1): 'A', ('ih', 0, 1, 1, 0): 'V', ('ih', 0, 1, 1, 1): 'S', ('mode', 1, 1, 1): 'C', ('ih', 1, 1, 1, 0): 'V', ('ih', 1, 1, 1, 1): 'V', ('c2', 0, 0, 0): 'S', ('c2', 0, 0, 1): 'S', ('c2', 0, 0, 2): 'S', ('c2', 0, 0, 3): 'S', ('c2', 1, 0, 0): 'S', ('c2', 1, 0, 1): 'S', ('c2', 1, 0, 2): 'S', ('c2', 1, 0, 3): 'S', ('mx', 0, 0, 0, 0): 'V', ('mx', 0, 0, 0, 1): 'V', ('mx', 0, 0, 0, 2): 'S', ('mx', 0, 0, 0, 3): 'V', ('mx', 1, 0, 0, 0): 'V', ('mx', 1, 0, 0, 1): 'S', ('mx', 1, 0, 0, 2): 'V', ('mx', 1, 0, 0, 3): 'S', ('c2', 0, 1, 0): 'S', ('c2', 0, 1, 1): 'S', ('c2', 0, 1, 2): 'S', ('c2', 0, 1, 3): 'S', ('c2', 1, 1, 0): 'S', ('c2', 1, 1, 1): 'S', ('c2', 1, 1, 2): 'S', ('c2', 1, 1, 3): 'S', ('mx', 0, 1, 0, 0): 'V', ('mx', 0, 1, 0, 1): 'V', ('mx', 0, 1, 0, 2): 'S', ('mx', 0, 1, 0, 3): 'S', ('mx', 1, 1, 0, 0): 'V', ('mx', 1, 1, 0, 1): 'S', ('mx', 1, 1, 0, 2): 'S', ('mx', 1, 1, 0, 3): 'V', ('val', 0, 0, 0): 'S', ('val', 0, 0, 1): 'S', ('mx', 0, 1, 1, 0): 'V', ('mx', 0, 1, 1, 1): 'V', ('mx', 0, 1, 1, 2): 'S', ('mx', 0, 1, 1, 3): 'V', ('mx', 1, 1, 1, 0): 'V', ('mx', 1, 1, 1, 1): 'S', ('mx', 1, 1, 1, 2): 'S', ('mx', 1, 1, 1, 3): 'S', ('val', 1, 0, 0): 'S', ('val', 1, 0, 1): 'S', ('val', 1, 1, 0): 'V', ('val', 1, 1, 1): 'S'}
         xT_planes = xT.rearrange("(a p i) t -> a i p t", p=P, i=PACK)
-        w1_rows = w1.rearrange("(a p j) c -> a p j c", p=P, j=PACK)
-        tiles = {}
-
-        def copy_on(engine, dst, src):
-            if engine == "S":
-                nc.scalar.copy(out=dst, in_=src)
-            elif engine == "G":
-                nc.gpsimd.tensor_scalar(out=dst, in0=src, scalar1=1.0, scalar2=0.0, op0=MULT, op1=ADD)
-            else:
-                nc.vector.tensor_copy(out=dst, in_=src)
-
-        def add_bias(engine, dst, acc, bias):
-            if engine == "S":
-                nc.scalar.activation(out=dst, in_=acc, func=IDENT, bias=bias)
-            else:
-                nc.vector.tensor_scalar(out=dst, in0=acc, scalar1=bias, scalar2=None, op0=ADD)
+        w1_rows = w1.rearrange("(a p i) r -> a p i r", p=P, i=PACK)
+        window, w1_loaded, picked = {}, {}, {}
+        x_rounded, w1_rounded, h_rounded = {}, {}, {}
+        x_mx, w1_mx, h_mx = {}, {}, {}
+        c2_biased, larger = {}, {}
 
         def load_scale_rows(plane, scales):
-            for q in range(4):
+            for quadrant in range(4):
                 nc.sync.dma_start(
-                    out=plane[32 * q : 32 * q + 4, :, :].bitcast(I32),
-                    in_=scales[:, 4 * q : 4 * q + 4, :].rearrange("a r c -> r a c").bitcast(I32),
+                    out=plane[32 * quadrant : 32 * quadrant + 4, :, :].bitcast(I32),
+                    in_=scales[:, 4 * quadrant : 4 * quadrant + 4, :].rearrange("g q c -> q g c").bitcast(I32),
                 )
 
-        def quantise(op, rounded, width):
-            name = "%s%d%d%d" % (op[0], op[1], op[2], op[3] if len(op) > 3 else 0)
+        def load_window(a, i):
+            window[a, i] = windows.tile([P, T], F32, name="window")
+            nc.sync.dma_start(out=window[a, i][:], in_=xT_planes[a, i])
+
+        def load_w1(a, b):
+            w1_loaded[a, b] = quarters.tile([P, PACK, BANK], F32, name="w1_loaded")
+            nc.sync.dma_start(out=w1_loaded[a, b][:], in_=w1_rows[a, :, :, BANK * b : BANK * (b + 1)])
+
+        def load_unit_bias(bias_sb, bias):
+            nc.sync.dma_start(out=bias_sb[:], in_=bias.rearrange("(b p t) -> p b t", p=P, t=PACK))
+
+        def copy(engine, dst, src):
+            if engine is scalar:
+                scalar.copy(out=dst, in_=src)
+            else:
+                vector.tensor_copy(out=dst, in_=src)
+
+        def add_bias(engine, dst, acc, bias):
+            if engine is scalar:
+                scalar.activation(out=dst, in_=acc, func=IDENTITY, bias=bias)
+            else:
+                vector.tensor_scalar(out=dst, in0=acc, scalar1=bias, scalar2=None, op0=ADD)
+
+        def staged(tiles, key, name):
+            if key not in tiles:
+                tiles[key] = staging.tile([P, PACK * BANK], BF16, name=name, align_bytes=64)
+            return tiles[key]
+
+        def interleave(engine, dst, rows, width, part):
+            lo, hi = part[0] * width // 2, part[1] * width // 2
+            copy(
+                engine,
+                dst[:, PACK * lo : PACK * hi].rearrange("p (c n u) -> p c u n", n=RUN, u=PACK),
+                rows[:, :, lo:hi].rearrange("p u (c n) -> p c u n", n=RUN),
+            )
+
+        def quantise(name, rounded, width):
             codes = keep.tile([P, width], U32, name=name + "_codes", align_bytes=64)
             plane = keep.tile([P, width], U8, name=name + "_plane", align_bytes=64)
-            nc.vector.quantize_mx(out=codes[:].bitcast(FP8X4), scales=plane[:], in_=rounded[:, 0 : PACK * width])
-            tiles[op] = (codes, plane)
+            vector.quantize_mx(out=codes[:].bitcast(FP8X4), scales=plane[:], in_=rounded[:, 0 : PACK * width])
+            return codes, plane
 
-        nc.vector.memset(w2_sraw[:].bitcast(U32), 0)
-        nc.vector.memset(w3_plane[:].bitcast(U32), 0)
-        for op in ORDER:
-            k = op[0]
-            if op == ("ld", "offs"):
-                nc.sync.dma_start(offsets[:], offs)
-            elif op == ("ld", "w2s"):
-                load_scale_rows(w2_sraw, w2_scales)
-            elif op == ("ld", "w2"):
-                nc.sync.dma_start(out=w2_raw[:].bitcast(I32), in_=w2_words.rearrange("a p c -> p a c").bitcast(I32))
-            elif op == ("ld", "w3"):
-                nc.sync.dma_start(out=w3_codes[:].bitcast(I32), in_=w3_words.rearrange("a p n t -> p a (n t)").bitcast(I32))
-                load_scale_rows(w3_plane, w3_scales)
-            elif k == "ld" and op[1] == "wgt":
-                nc.sync.dma_start(out=wgt_sb[op[2]][:], in_=wgt[:, W * op[2] : W * (op[2] + 1)])
-            elif k == "ld" and op[1] == "win":
-                tiles[op] = windows.tile([P, T], F32, name="window")
-                nc.sync.dma_start(out=tiles[op][:], in_=xT_planes[op[2], op[3]])
-                if op[2:] == (0, 1):
-                    nc.sync.dma_start(out=b2_sb[:], in_=b2.rearrange("(b p t) -> p b t", p=P, t=PACK))
-                if op[2:] == (0, 2):
-                    nc.sync.dma_start(out=b1_sb[:], in_=b1.rearrange("(b p t) -> p b t", p=P, t=PACK))
-                if op[2:] == (0, 3):
-                    with nc.allow_non_contiguous_dma(reason="one bias value a partition"):
-                        nc.sync.dma_start(out=b3_sb[:], in_=b3.rearrange("(c p) -> p c", p=P))
-            elif k == "ld":
-                a, b = op[2:]
-                tiles[op] = ring4.tile([P, PACK, W], F32, name="w1_raw")
-                nc.sync.dma_start(out=tiles[op][:], in_=w1_rows[a, :, :, W * b : W * (b + 1)])
-            elif op == ("perm", "w2"):
-                nc.vector.tensor_copy(
-                    out=w2_codes[:].bitcast(U16).rearrange("p (g t m) -> p g t m", t=PACK, m=P),
-                    in_=w2_raw[:].rearrange("p a c -> p (a c)").bitcast(U16).rearrange("p (g m t) -> p g t m", t=PACK, m=P),
+        def two_passes(width, stationary, moving):
+            acc = psum.tile([P, BANK], F32, name="acc")
+            for g in range(2):
+                nc.tensor.matmul_mx(
+                    out=acc[:, 0:width],
+                    lhsT=stationary[g][0],
+                    lhsT_scale=stationary[g][1],
+                    rhs=moving[g][0],
+                    rhs_scale=moving[g][1],
+                    start=(g == 0),
+                    stop=(g == 1),
                 )
-            elif op == ("perm", "w2s"):
-                nc.vector.tensor_copy(
-                    out=w2_plane[:].rearrange("p (g t m) -> p g t m", t=PACK, m=P),
-                    in_=w2_sraw[:].rearrange("p a (b m t) -> p (a b) t m", t=PACK, m=P),
+            return acc[:, 0:width]
+
+        def columns(operand, cols):
+            codes, plane = operand
+            return codes[:, cols].bitcast(FP8X4), plane[:, cols]
+
+        def gather_both(a, i):
+            for s in range(2):
+                if (a, s) not in picked:
+                    picked[a, s] = quarters.tile([P, PACK, BANK], F32, name="picked")
+                picks = offsets[:, LIST_COLUMNS * s : LIST_COLUMNS * (s + 1)]
+                vector.tensor_tensor(picked[a, s][:, i, :], window[a, i][:].indirect(picks), wgt_sb[s][:], MULT)
+
+        def round_x(engine, a, s, part):
+            interleave(engine, staged(x_rounded, (a, s), "x_rounded"), picked[a, s], BANK, part)
+
+        def quantise_x(a, s):
+            x_mx[a, s] = quantise("x%d%d" % (a, s), x_rounded[a, s], BANK)
+
+        def round_w1(engine, a, b, part):
+            lo, hi = part[0] * P // 2, part[1] * P // 2
+            dst = staged(w1_rounded, (a, b), "w1_rounded")
+            copy(
+                engine,
+                dst[:].rearrange("p (t m i) -> p m i t", t=PACK, i=PACK)[:, lo:hi, :, :],
+                w1_loaded[a, b][:, :, PACK * lo : PACK * hi].rearrange("p i (m t) -> p m i t", t=PACK),
+            )
+
+        def quantise_w1(a, b):
+            w1_mx[a, b] = quantise("w1_%d%d" % (a, b), w1_rounded[a, b], BANK)
+
+        def critic2(engine, b, s, outputs):
+            if (b, s) not in c2_biased:
+                c2_biased[b, s] = critic2_sums.tile([P, PACK, BANK], F32, name="c2_biased")
+            for t in outputs:
+                first = [H * a + BANK * b + P * t for a in range(2)]
+                weights = [(w2_codes[:, 2 * c : 2 * (c + P)].bitcast(FP4X4), w2_plane[:, c : c + P]) for c in first]
+                acc = two_passes(BANK, weights, [columns(x_mx[a, s], slice(0, BANK)) for a in range(2)])
+                add_bias(engine, c2_biased[b, s][:, t, :], acc, b2_sb[:, b, t : t + 1])
+
+        def place(span):
+            s, lo = divmod(span[0], BANK)
+            return s, slice(lo, lo + span[1])
+
+        def critic1(b, span, t):
+            s, cols = place(span)
+            weights = [columns(w1_mx[a, b], slice(P * t, P * (t + 1))) for a in range(2)]
+            return two_passes(span[1], weights, [columns(x_mx[a, s], cols) for a in range(2)])
+
+        def maxout(b, span, outputs):
+            s, cols = place(span)
+            if (b, span) not in larger:
+                larger[b, span] = staging.tile([P, PACK, BANK], BF16, name="larger")
+            for t in outputs:
+                vector.scalar_tensor_tensor(
+                    out=larger[b, span][:, t, 0 : span[1]],
+                    in0=critic1(b, span, t),
+                    scalar=b1_sb[:, b, t : t + 1],
+                    in1=c2_biased[b, s][:, t, cols],
+                    op0=ADD,
+                    op1=MAX,
                 )
-            elif k == "g":
-                a, i, s = op[1:]
-                if ("picked", a, s) not in tiles:
-                    tiles[("picked", a, s)] = ring4.tile([P, PACK, W], F32, name="picked")
-                nc.vector.tensor_tensor(
-                    tiles[("picked", a, s)][:, i, :],
-                    tiles[("ld", "win", a, i)][:].indirect(offsets[:, 32 * s : 32 * (s + 1)]),
-                    wgt_sb[s][:],
-                    MULT,
-                )
-            elif k == "ix":
-                a, s, h = op[1:]
-                if op[:3] not in tiles:
-                    tiles[op[:3]] = ring2.tile([P, PACK * W], BF16, name="x_rounded", align_bytes=64)
-                copy_on(
-                    ASG[op],
-                    tiles[op[:3]][:, 1024 * h : 1024 * (h + 1)].rearrange("p (c i t) -> p c t i", i=4, t=PACK),
-                    tiles[("picked", a, s)][:, :, 256 * h : 256 * (h + 1)].rearrange("p t (c i) -> p c t i", i=4),
-                )
-            elif k == "iw":
-                a, b, h = op[1:]
-                if op[:3] not in tiles:
-                    tiles[op[:3]] = ring2.tile([P, PACK * W], BF16, name="w1_rounded", align_bytes=64)
-                copy_on(
-                    ASG[op],
-                    tiles[op[:3]][:].rearrange("p (t m j) -> p m j t", t=PACK, j=PACK)[:, 64 * h : 64 * (h + 1), :, :],
-                    tiles[("ld", "w1raw", a, b)][:, :, 256 * h : 256 * (h + 1)].rearrange("p j (m t) -> p m j t", t=PACK),
-                )
-            elif k == "ih":
-                b, s, q, h = op[1:]
-                half = W // NCH[(b, s)] // 2
-                if op[:4] not in tiles:
-                    tiles[op[:4]] = ring2.tile([P, PACK * W], BF16, name="h_rounded", align_bytes=64)
-                if ASG[("mode",) + op[1:4]] == "C":
-                    lo = 2 * half * q + half * h
-                    nc.vector.tensor_tensor(
-                        tiles[op[:4]][:, PACK * half * h : PACK * half * (h + 1)].rearrange("p (c i t) -> p c t i", i=2, t=PACK),
-                        tiles[("mx", b, s, q)][:, :, half * h : half * (h + 1)].rearrange("p t (c i) -> p c t i", i=2),
-                        tiles[("c2", b, s)][:, :, lo : lo + half].rearrange("p t (c i) -> p c t i", i=2),
-                        MAX,
-                    )
-                    continue
-                copy_on(
-                    ASG[op],
-                    tiles[op[:4]][:, PACK * half * h : PACK * half * (h + 1)].rearrange("p (c i t) -> p c t i", i=4, t=PACK),
-                    tiles[("mx", b, s, q)][:, :, half * h : half * (h + 1)].rearrange("p t (c i) -> p c t i", i=4),
-                )
-            elif k == "qx":
-                quantise(op, tiles[("ix",) + op[1:]], W)
-            elif k == "qw":
-                quantise(op, tiles[("iw",) + op[1:]], W)
-            elif k == "qh":
-                quantise(op, tiles[("ih",) + op[1:]], W // NCH[op[1:3]])
-            elif k == "c2":
-                b, s = op[1:3]
-                if op[:3] not in tiles:
-                    tiles[op[:3]] = ring3.tile([P, PACK, W], F32, name="c2")
-                sums = tiles[op[:3]]
-                for t in op[3:]:
-                    acc = psum.tile([P, W], F32, name="acc")
-                    for a in range(2):
-                        col = H * a + W * b + P * t
-                        nc.tensor.matmul_mx(
-                            out=acc[:],
-                            lhsT=w2_codes[:, 2 * col : 2 * (col + P)].bitcast(FP4X4),
-                            lhsT_scale=w2_plane[:, col : col + P],
-                            rhs=tiles[("qx", a, s)][0][:].bitcast(FP8X4),
-                            rhs_scale=tiles[("qx", a, s)][1][:],
-                            start=(a == 0),
-                            stop=(a == 1),
-                        )
-                    add_bias(ASG[op], sums[:, t, :], acc[:], b2_sb[:, b, t : t + 1])
-            elif k == "mx":
-                b, s, q = op[1:4]
-                width = W // NCH[(b, s)]
-                cols = slice(width * q, width * (q + 1))
-                if op[:4] not in tiles:
-                    if ASG[("mode",) + op[1:4]] == "A":
-                        tiles[op[:4]] = ring2.tile([P, PACK, W], BF16, name="larger")
-                    else:
-                        tiles[op[:4]] = ring2.tile([P, PACK, width], F32, name="c1")
-                larger = tiles[op[:4]]
-                for t in op[4:]:
-                    acc = psum.tile([P, W], F32, name="acc")
-                    for a in range(2):
-                        nc.tensor.matmul_mx(
-                            out=acc[:, 0:width],
-                            lhsT=tiles[("qw", a, b)][0][:, P * t : P * (t + 1)].bitcast(FP8X4),
-                            lhsT_scale=tiles[("qw", a, b)][1][:, P * t : P * (t + 1)],
-                            rhs=tiles[("qx", a, s)][0][:, cols].bitcast(FP8X4),
-                            rhs_scale=tiles[("qx", a, s)][1][:, cols],
-                            start=(a == 0),
-                            stop=(a == 1),
-                        )
-                    if ASG[("mode",) + op[1:4]] == "C":
-                        add_bias(ASG[op], larger[:, t, :], acc[:, 0:width], b1_sb[:, b, t : t + 1])
-                        continue
-                    nc.vector.scalar_tensor_tensor(
-                        out=larger[:, t, 0:width], in0=acc[:, 0:width], scalar=b1_sb[:, b, t : t + 1],
-                        in1=tiles[("c2", b, s)][:, t, cols], op0=ADD, op1=MAX
-                    )
-            elif k == "val":
-                s, q = op[1:3]
-                n = max(NCH[(0, s)], NCH[(1, s)])
-                width = W // n
-                for c in op[3:]:
-                    acc = psum.tile([P, W], F32, name="acc")
-                    for b in range(2):
-                        nb = NCH[(b, s)]
-                        codes, plane = tiles[("qh", b, s, q * nb // n)]
-                        lo = width * q if nb < n else 0
-                        nc.tensor.matmul_mx(
-                            out=acc[:, 0:width],
-                            lhsT=w3_codes[:, b, P * c : P * (c + 1)].bitcast(FP8X4),
-                            lhsT_scale=w3_plane[:, b, P * c : P * (c + 1)],
-                            rhs=codes[:, lo : lo + width].bitcast(FP8X4),
-                            rhs_scale=plane[:, lo : lo + width],
-                            start=(b == 0),
-                            stop=(b == 1),
-                        )
-                    result = keep.tile([P, W], F32, name="result%d%d%d" % op[1:])
-                    add_bias(ASG[op], result[:, 0:width], acc[:, 0:width], b3_sb[:, c : c + 1])
-                    nc.sync.dma_start(
-                        out=out[P * c : P * (c + 1), W * s + width * q : W * s + width * (q + 1)], in_=result[:, 0:width]
-                    )
+
+        def critic1_by_scalar(b, span):
+            c1_biased = keep.tile([P, PACK, span[1]], F32, name="c1_biased")
+            for t in ALL_T:
+                add_bias(scalar, c1_biased[:, t, :], critic1(b, span, t), b1_sb[:, b, t : t + 1])
+            return c1_biased
+
+        def maxout_interleaved(b, span, c1_biased):
+            s, cols = place(span)
+            dst = staged(h_rounded, (b, span), "h_rounded")
+            vector.tensor_tensor(
+                dst[:, 0 : PACK * span[1]].rearrange("p (c n t) -> p c t n", n=2, t=PACK),
+                c1_biased[:].rearrange("p t (c n) -> p c t n", n=2),
+                c2_biased[b, s][:, :, cols].rearrange("p t (c n) -> p c t n", n=2),
+                MAX,
+            )
+
+        def interleave_h(engine, b, span, part):
+            interleave(engine, staged(h_rounded, (b, span), "h_rounded"), larger[b, span], span[1], part)
+
+        def quantise_h(b, span):
+            h_mx[b, span] = quantise("h%d_%d" % (b, span[0]), h_rounded[b, span], span[1])
+
+        def values(engine, span, c):
+            start, width = span
+            actions = slice(P * c, P * (c + 1))
+            weights = [(w3_codes[:, b, actions].bitcast(FP8X4), w3_plane[:, b, actions]) for b in range(2)]
+            acc = two_passes(width, weights, [columns(h_mx[b, span], slice(0, width)) for b in range(2)])
+            result = keep.tile([P, width], F32, name="result%d_%d" % (start, c))
+            add_bias(engine, result[:], acc, b3_sb[:, c : c + 1])
+            nc.sync.dma_start(out=out[actions, start : start + width], in_=result[:])
+
+        vector.memset(w2_plane_loaded[:].bitcast(U32), 0)
+        vector.memset(w3_plane[:].bitcast(U32), 0)
+
+        nc.sync.dma_start(offsets[:], offs)
+        load_scale_rows(w2_plane_loaded, w2_scales)
+        nc.sync.dma_start(out=w2_loaded[:].bitcast(I32), in_=w2_words.rearrange("a p c -> p a c").bitcast(I32))
+        nc.sync.dma_start(out=wgt_sb[0][:], in_=wgt[:, 0:BANK])
+        load_window(0, 0)
+        nc.sync.dma_start(out=wgt_sb[1][:], in_=wgt[:, BANK : 2 * BANK])
+        vector.tensor_copy(
+            out=w2_codes[:].bitcast(U16).rearrange("p (g t m) -> p g t m", t=PACK, m=P),
+            in_=w2_loaded[:].rearrange("p a c -> p (a c)").bitcast(U16).rearrange("p (g m t) -> p g t m", t=PACK, m=P),
+        )
+        vector.tensor_copy(
+            out=w2_plane[:].rearrange("p (g t m) -> p g t m", t=PACK, m=P),
+            in_=w2_plane_loaded[:].rearrange("p a (b m t) -> p (a b) t m", t=PACK, m=P),
+        )
+
+        load_window(0, 1)
+        load_unit_bias(b2_sb, b2)
+        gather_both(0, 0)
+        load_window(0, 2)
+        load_unit_bias(b1_sb, b1)
+        load_window(0, 3)
+        with nc.allow_non_contiguous_dma(reason="b3_sb[p, c] is the bias of action 128 c + p"):
+            nc.sync.dma_start(out=b3_sb[:], in_=b3.rearrange("(c p) -> p c", p=P))
+        gather_both(0, 1)
+        load_window(1, 0)
+        gather_both(0, 2)
+        gather_both(0, 3)
+
+        round_x(scalar, 0, 0, WHOLE)
+        load_window(1, 1)
+        gather_both(1, 0)
+        round_x(scalar, 0, 1, WHOLE)
+        load_w1(0, 0)
+        load_window(1, 2)
+        quantise_x(0, 0)
+        gather_both(1, 1)
+        quantise_x(0, 1)
+        round_w1(scalar, 0, 0, WHOLE)
+        gather_both(1, 2)
+        load_window(1, 3)
+        gather_both(1, 3)
+
+        quantise_w1(0, 0)
+        load_w1(1, 0)
+        round_w1(vector, 1, 0, WHOLE)
+        load_w1(0, 1)
+        load_w1(1, 1)
+        round_x(scalar, 1, 0, WHOLE)
+        round_x(scalar, 1, 1, LOWER)
+        round_w1(scalar, 0, 1, LOWER)
+        quantise_x(1, 0)
+        quantise_w1(1, 0)
+        critic2(scalar, 0, 0, (0, 1, 2))
+        round_w1(vector, 0, 1, UPPER)
+        critic2(scalar, 1, 0, (0,))
+        round_x(vector, 1, 1, UPPER)
+        critic2(vector, 0, 0, (3,))
+        quantise_x(1, 1)
+        round_w1(vector, 1, 1, LOWER)
+        maxout(0, SPAN_0, (0, 1))
+        quantise_w1(0, 1)
+        round_w1(scalar, 1, 1, UPPER)
+        quantise_w1(1, 1)
+        critic2(scalar, 1, 0, (1, 2, 3))
+        maxout(0, SPAN_0, (2, 3))
+        critic2(scalar, 0, 1, (0, 1, 2))
+        maxout(1, SPAN_0, ALL_T)
+
+        interleave_h(scalar, 0, SPAN_0, LOWER)
+        interleave_h(scalar, 1, SPAN_0, LOWER)
+        interleave_h(vector, 0, SPAN_0, UPPER)
+        critic2(scalar, 0, 1, (3,))
+        interleave_h(vector, 1, SPAN_0, UPPER)
+        quantise_h(0, SPAN_0)
+        maxout(0, SPAN_1, ALL_T)
+        quantise_h(1, SPAN_0)
+        critic2(scalar, 1, 1, ALL_T)
+        nc.sync.dma_start(out=w3_codes[:].bitcast(I32), in_=w3_words.rearrange("b p n t -> p b (n t)").bitcast(I32))
+        load_scale_rows(w3_plane, w3_scales)
+        interleave_h(scalar, 0, SPAN_1, LOWER)
+        maxout(1, SPAN_1, ALL_T)
+        interleave_h(scalar, 1, SPAN_1, LOWER)
+        interleave_h(vector, 0, SPAN_1, UPPER)
+        interleave_h(vector, 1, SPAN_1, UPPER)
+
+        maxout(1, SPAN_2, ALL_T)
+        c1_biased = critic1_by_scalar(0, SPAN_2)
+        quantise_h(0, SPAN_1)
+        quantise_h(1, SPAN_1)
+        maxout_interleaved(0, SPAN_2, c1_biased)
+        values(scalar, SPAN_0, 0)
+        values(scalar, SPAN_0, 1)
+        interleave_h(vector, 1, SPAN_2, LOWER)
+        quantise_h(0, SPAN_2)
+        interleave_h(scalar, 1, SPAN_2, UPPER)
+        quantise_h(1, SPAN_2)
+        values(scalar, SPAN_1, 0)
+        values(scalar, SPAN_1, 1)
+        values(vector, SPAN_2, 0)
+        values(scalar, SPAN_2, 1)

from contextlib import ExitStack

import concourse.mybir as mybir

K, T, S, H, N = 1024, 2048, 1024, 1024, 256
FLOPS = 2 * S * (2 * K * H + H * N)

F32 = mybir.dt.float32
BF16 = mybir.dt.bfloat16
I32 = mybir.dt.int32
U32 = mybir.dt.uint32
U16 = mybir.dt.uint16
U8 = mybir.dt.uint8
FP8X4 = mybir.dt.float8_e4m3fn_x4
FP4X4 = mybir.dt.float4_e2m1fn_x4
MULT = mybir.AluOpType.mult
ADD = mybir.AluOpType.add
MAX = mybir.AluOpType.max
IDENTITY = mybir.ActivationFunctionType.Identity

P = 128
PACK = 4
BANK = 512
LIST_COLUMNS = BANK // 16
RUN = 4

SPAN_0, SPAN_1, SPAN_2 = (0, 512), (512, 256), (768, 256)

WHOLE, LOWER, UPPER = (0, 2), (0, 1), (1, 2)
ALL_T = range(PACK)


def tile_list_replay_maxout_values_kernel(
    tc, xT, wgt, offs, w1, b1, w2_words, w2_scales, b2, w3_words, w3_scales, b3, out
):
    nc = tc.nc
    vector, scalar = nc.vector, nc.scalar
    with ExitStack() as ctx:
        keep = ctx.enter_context(tc.tile_pool(name="keep", bufs=1))
        windows = ctx.enter_context(tc.tile_pool(name="windows", bufs=6))
        critic2_sums = ctx.enter_context(tc.tile_pool(name="critic2_sums", bufs=3))
        staging = ctx.enter_context(tc.tile_pool(name="staging", bufs=2))
        quarters = ctx.enter_context(tc.tile_pool(name="quarters", bufs=4))
        psum = ctx.enter_context(tc.psum_pool(name="psum", bufs=8))

        offsets = keep.tile([P, S // 16], U16, name="offsets")
        wgt_sb = [keep.tile([P, BANK], F32, name="wgt%d" % s) for s in range(2)]
        w2_loaded = keep.tile([P, 2, 2 * H], U8, name="w2_loaded", align_bytes=64)
        w2_codes = keep.tile([P, 2 * 2 * H], U8, name="w2_codes", align_bytes=64)
        w2_plane_loaded = keep.tile([P, 2, H], U8, name="w2_plane_loaded", align_bytes=64)
        w2_plane = keep.tile([P, 2 * H], U8, name="w2_plane", align_bytes=64)
        w3_codes = keep.tile([P, 2, N], U32, name="w3_codes", align_bytes=64)
        w3_plane = keep.tile([P, 2, N], U8, name="w3_plane", align_bytes=64)
        b1_sb = keep.tile([P, 2, PACK], F32, name="b1_sb")
        b2_sb = keep.tile([P, 2, PACK], F32, name="b2_sb")
        b3_sb = keep.tile([P, 2], F32, name="b3_sb")

        xT_planes = xT.rearrange("(a p i) t -> a i p t", p=P, i=PACK)
        w1_rows = w1.rearrange("(a p i) r -> a p i r", p=P, i=PACK)
        window, w1_loaded, picked = {}, {}, {}
        x_rounded, w1_rounded, h_rounded = {}, {}, {}
        x_mx, w1_mx, h_mx = {}, {}, {}
        c2_biased, larger = {}, {}

        def load_scale_rows(plane, scales):
            for quadrant in range(4):
                nc.sync.dma_start(
                    out=plane[32 * quadrant : 32 * quadrant + 4, :, :].bitcast(I32),
                    in_=scales[:, 4 * quadrant : 4 * quadrant + 4, :].rearrange("g q c -> q g c").bitcast(I32),
                )

        def load_window(a, i):
            window[a, i] = windows.tile([P, T], F32, name="window")
            nc.sync.dma_start(out=window[a, i][:], in_=xT_planes[a, i])

        def load_w1(a, b):
            w1_loaded[a, b] = quarters.tile([P, PACK, BANK], F32, name="w1_loaded")
            nc.sync.dma_start(out=w1_loaded[a, b][:], in_=w1_rows[a, :, :, BANK * b : BANK * (b + 1)])

        def load_unit_bias(bias_sb, bias):
            nc.sync.dma_start(out=bias_sb[:], in_=bias.rearrange("(b p t) -> p b t", p=P, t=PACK))

        def copy(engine, dst, src):
            if engine is scalar:
                scalar.copy(out=dst, in_=src)
            else:
                vector.tensor_copy(out=dst, in_=src)

        def add_bias(engine, dst, acc, bias):
            if engine is scalar:
                scalar.activation(out=dst, in_=acc, func=IDENTITY, bias=bias)
            else:
                vector.tensor_scalar(out=dst, in0=acc, scalar1=bias, scalar2=None, op0=ADD)

        def staged(tiles, key, name):
            if key not in tiles:
                tiles[key] = staging.tile([P, PACK * BANK], BF16, name=name, align_bytes=64)
            return tiles[key]

        def interleave(engine, dst, rows, width, part):
            lo, hi = part[0] * width // 2, part[1] * width // 2
            copy(
                engine,
                dst[:, PACK * lo : PACK * hi].rearrange("p (c n u) -> p c u n", n=RUN, u=PACK),
                rows[:, :, lo:hi].rearrange("p u (c n) -> p c u n", n=RUN),
            )

        def quantise(name, rounded, width):
            codes = keep.tile([P, width], U32, name=name + "_codes", align_bytes=64)
            plane = keep.tile([P, width], U8, name=name + "_plane", align_bytes=64)
            vector.quantize_mx(out=codes[:].bitcast(FP8X4), scales=plane[:], in_=rounded[:, 0 : PACK * width])
            return codes, plane

        def two_passes(width, stationary, moving):
            acc = psum.tile([P, BANK], F32, name="acc")
            for g in range(2):
                nc.tensor.matmul_mx(
                    out=acc[:, 0:width],
                    lhsT=stationary[g][0],
                    lhsT_scale=stationary[g][1],
                    rhs=moving[g][0],
                    rhs_scale=moving[g][1],
                    start=(g == 0),
                    stop=(g == 1),
                )
            return acc[:, 0:width]

        def columns(operand, cols):
            codes, plane = operand
            return codes[:, cols].bitcast(FP8X4), plane[:, cols]

        def gather_both(a, i):
            for s in range(2):
                if (a, s) not in picked:
                    picked[a, s] = quarters.tile([P, PACK, BANK], F32, name="picked")
                picks = offsets[:, LIST_COLUMNS * s : LIST_COLUMNS * (s + 1)]
                vector.tensor_tensor(picked[a, s][:, i, :], window[a, i][:].indirect(picks), wgt_sb[s][:], MULT)

        def round_x(engine, a, s, part):
            interleave(engine, staged(x_rounded, (a, s), "x_rounded"), picked[a, s], BANK, part)

        def quantise_x(a, s):
            x_mx[a, s] = quantise("x%d%d" % (a, s), x_rounded[a, s], BANK)

        def round_w1(engine, a, b, part):
            lo, hi = part[0] * P // 2, part[1] * P // 2
            dst = staged(w1_rounded, (a, b), "w1_rounded")
            copy(
                engine,
                dst[:].rearrange("p (t m i) -> p m i t", t=PACK, i=PACK)[:, lo:hi, :, :],
                w1_loaded[a, b][:, :, PACK * lo : PACK * hi].rearrange("p i (m t) -> p m i t", t=PACK),
            )

        def quantise_w1(a, b):
            w1_mx[a, b] = quantise("w1_%d%d" % (a, b), w1_rounded[a, b], BANK)

        def critic2(engine, b, s, outputs):
            if (b, s) not in c2_biased:
                c2_biased[b, s] = critic2_sums.tile([P, PACK, BANK], F32, name="c2_biased")
            for t in outputs:
                first = [H * a + BANK * b + P * t for a in range(2)]
                weights = [(w2_codes[:, 2 * c : 2 * (c + P)].bitcast(FP4X4), w2_plane[:, c : c + P]) for c in first]
                acc = two_passes(BANK, weights, [columns(x_mx[a, s], slice(0, BANK)) for a in range(2)])
                add_bias(engine, c2_biased[b, s][:, t, :], acc, b2_sb[:, b, t : t + 1])

        def place(span):
            s, lo = divmod(span[0], BANK)
            return s, slice(lo, lo + span[1])

        def critic1(b, span, t):
            s, cols = place(span)
            weights = [columns(w1_mx[a, b], slice(P * t, P * (t + 1))) for a in range(2)]
            return two_passes(span[1], weights, [columns(x_mx[a, s], cols) for a in range(2)])

        def maxout(b, span, outputs):
            s, cols = place(span)
            if (b, span) not in larger:
                larger[b, span] = staging.tile([P, PACK, BANK], BF16, name="larger")
            for t in outputs:
                vector.scalar_tensor_tensor(
                    out=larger[b, span][:, t, 0 : span[1]],
                    in0=critic1(b, span, t),
                    scalar=b1_sb[:, b, t : t + 1],
                    in1=c2_biased[b, s][:, t, cols],
                    op0=ADD,
                    op1=MAX,
                )

        def critic1_by_scalar(b, span):
            c1_biased = keep.tile([P, PACK, span[1]], F32, name="c1_biased")
            for t in ALL_T:
                add_bias(scalar, c1_biased[:, t, :], critic1(b, span, t), b1_sb[:, b, t : t + 1])
            return c1_biased

        def maxout_interleaved(b, span, c1_biased):
            s, cols = place(span)
            dst = staged(h_rounded, (b, span), "h_rounded")
            vector.tensor_tensor(
                dst[:, 0 : PACK * span[1]].rearrange("p (c n t) -> p c t n", n=2, t=PACK),
                c1_biased[:].rearrange("p t (c n) -> p c t n", n=2),
                c2_biased[b, s][:, :, cols].rearrange("p t (c n) -> p c t n", n=2),
                MAX,
            )

        def interleave_h(engine, b, span, part):
            interleave(engine, staged(h_rounded, (b, span), "h_rounded"), larger[b, span], span[1], part)

        def quantise_h(b, span):
            h_mx[b, span] = quantise("h%d_%d" % (b, span[0]), h_rounded[b, span], span[1])

        def values(engine, span, c):
            start, width = span
            actions = slice(P * c, P * (c + 1))
            weights = [(w3_codes[:, b, actions].bitcast(FP8X4), w3_plane[:, b, actions]) for b in range(2)]
            acc = two_passes(width, weights, [columns(h_mx[b, span], slice(0, width)) for b in range(2)])
            result = keep.tile([P, width], F32, name="result%d_%d" % (start, c))
            add_bias(engine, result[:], acc, b3_sb[:, c : c + 1])
            nc.sync.dma_start(out=out[actions, start : start + width], in_=result[:])

        vector.memset(w2_plane_loaded[:].bitcast(U32), 0)
        vector.memset(w3_plane[:].bitcast(U32), 0)

        nc.sync.dma_start(offsets[:], offs)
        load_scale_rows(w2_plane_loaded, w2_scales)
        nc.sync.dma_start(out=w2_loaded[:].bitcast(I32), in_=w2_words.rearrange("a p c -> p a c").bitcast(I32))
        nc.sync.dma_start(out=wgt_sb[0][:], in_=wgt[:, 0:BANK])
        load_window(0, 0)
        nc.sync.dma_start(out=wgt_sb[1][:], in_=wgt[:, BANK : 2 * BANK])
        vector.tensor_copy(
            out=w2_codes[:].bitcast(U16).rearrange("p (g t m) -> p g t m", t=PACK, m=P),
            in_=w2_loaded[:].rearrange("p a c -> p (a c)").bitcast(U16).rearrange("p (g m t) -> p g t m", t=PACK, m=P),
        )
        vector.tensor_copy(
            out=w2_plane[:].rearrange("p (g t m) -> p g t m", t=PACK, m=P),
            in_=w2_plane_loaded[:].rearrange("p a (b m t) -> p (a b) t m", t=PACK, m=P),
        )

        load_window(0, 1)
        load_unit_bias(b2_sb, b2)
        gather_both(0, 0)
        load_window(0, 2)
        load_unit_bias(b1_sb, b1)
        load_window(0, 3)
        with nc.allow_non_contiguous_dma(reason="b3_sb[p, c] is the bias of action 128 c + p"):
            nc.sync.dma_start(out=b3_sb[:], in_=b3.rearrange("(c p) -> p c", p=P))
        gather_both(0, 1)
        load_window(1, 0)
        gather_both(0, 2)
        gather_both(0, 3)

        round_x(scalar, 0, 0, WHOLE)
        load_window(1, 1)
        gather_both(1, 0)
        round_x(scalar, 0, 1, WHOLE)
        load_w1(0, 0)
        load_window(1, 2)
        quantise_x(0, 0)
        gather_both(1, 1)
        quantise_x(0, 1)
        round_w1(scalar, 0, 0, WHOLE)
        gather_both(1, 2)
        load_window(1, 3)
        gather_both(1, 3)

        quantise_w1(0, 0)
        load_w1(1, 0)
        round_w1(vector, 1, 0, WHOLE)
        load_w1(0, 1)
        load_w1(1, 1)
        round_x(scalar, 1, 0, WHOLE)
        round_x(scalar, 1, 1, LOWER)
        round_w1(scalar, 0, 1, LOWER)
        quantise_x(1, 0)
        quantise_w1(1, 0)
        critic2(scalar, 0, 0, (0, 1, 2))
        round_w1(vector, 0, 1, UPPER)
        critic2(scalar, 1, 0, (0,))
        round_x(vector, 1, 1, UPPER)
        critic2(vector, 0, 0, (3,))
        quantise_x(1, 1)
        round_w1(vector, 1, 1, LOWER)
        maxout(0, SPAN_0, (0, 1))
        quantise_w1(0, 1)
        round_w1(scalar, 1, 1, UPPER)
        quantise_w1(1, 1)
        critic2(scalar, 1, 0, (1, 2, 3))
        maxout(0, SPAN_0, (2, 3))
        critic2(scalar, 0, 1, (0, 1, 2))
        maxout(1, SPAN_0, ALL_T)

        interleave_h(scalar, 0, SPAN_0, LOWER)
        interleave_h(scalar, 1, SPAN_0, LOWER)
        interleave_h(vector, 0, SPAN_0, UPPER)
        critic2(scalar, 0, 1, (3,))
        interleave_h(vector, 1, SPAN_0, UPPER)
        quantise_h(0, SPAN_0)
        maxout(0, SPAN_1, ALL_T)
        quantise_h(1, SPAN_0)
        critic2(scalar, 1, 1, ALL_T)
        nc.sync.dma_start(out=w3_codes[:].bitcast(I32), in_=w3_words.rearrange("b p n t -> p b (n t)").bitcast(I32))
        load_scale_rows(w3_plane, w3_scales)
        interleave_h(scalar, 0, SPAN_1, LOWER)
        maxout(1, SPAN_1, ALL_T)
        interleave_h(scalar, 1, SPAN_1, LOWER)
        interleave_h(vector, 0, SPAN_1, UPPER)
        interleave_h(vector, 1, SPAN_1, UPPER)

        maxout(1, SPAN_2, ALL_T)
        c1_biased = critic1_by_scalar(0, SPAN_2)
        quantise_h(0, SPAN_1)
        quantise_h(1, SPAN_1)
        maxout_interleaved(0, SPAN_2, c1_biased)
        values(scalar, SPAN_0, 0)
        values(scalar, SPAN_0, 1)
        interleave_h(vector, 1, SPAN_2, LOWER)
        quantise_h(0, SPAN_2)
        interleave_h(scalar, 1, SPAN_2, UPPER)
        quantise_h(1, SPAN_2)
        values(scalar, SPAN_1, 0)
        values(scalar, SPAN_1, 1)
        values(vector, SPAN_2, 0)
        values(scalar, SPAN_2, 1)
